import numpy as np, ml_dtypes
CORES = [1,5,17,21,33,37,49,53]
N = 8
import mx_ref
BF = ml_dtypes.bfloat16
def gentries(a):
    return np.ascontiguousarray(a.reshape(8, 16, -1).transpose(0, 2, 1)).reshape(8, -1)
def gtable(e):
    e = np.asarray(e); return np.ascontiguousarray(e.reshape(8, -1, 16).transpose(0, 2, 1)).reshape(128, -1).astype(np.int32)
def gcols(t, e):
    v = np.concatenate([t.reshape(8, 16, -1, 4), np.zeros((8, 16, 1, 4), BF)], axis=2)
    return np.ascontiguousarray(np.stack([v[g][:, e[g]] for g in range(8)])).reshape(128, -1)
def tile(rs):
    return np.stack(rs, axis=2).reshape(128, -1).astype(BF)
def pick(q, e):
    c = np.concatenate([q[0].reshape(128, -1, 4), np.zeros((128, 1, 4), np.uint8)], axis=1); s = np.concatenate([q[1], np.ones((16, 1), np.uint8)], axis=1)
    return (np.ascontiguousarray(c[:, e].reshape(128, -1)), np.ascontiguousarray(s[:, e]))
def join(*qs):
    return (np.concatenate([q[0] for q in qs], axis=1), np.concatenate([q[1] for q in qs], axis=1))
def put(q, e, v):
    c, s = q[0].reshape(128, -1, 4).copy(), q[1].copy(); c[:, e] = v[0].reshape(128, -1, 4); s[:, e] = v[1]
    return (c.reshape(128, -1), s)
def pk(c, s):
    return (np.ascontiguousarray(c), mx_ref.live(s))
def emit(q):
    return q[0], q[1]
def packed(v, rng):
    q = [mx_ref.quantize(np.ascontiguousarray(v[r])) for r in range(N)]
    return np.stack([a for a, b in q]), np.stack([mx_ref.plane(b, rng) for a, b in q])
def values_of_codes():
    e, c = np.zeros((128, 128, 4), np.float32), np.zeros((128, 2, 4), np.uint8)
    e[np.arange(128), np.arange(128), 0] = 1
    c[:127, :, 0] = np.arange(256).reshape(2, 128).T[:127]
    return mx_ref.matmul(mx_ref.quantize(e.reshape(128, 512).astype(BF)), (c.reshape(128, 8), np.full((16, 2), 127, np.uint8))).T.reshape(-1).astype(np.float64)
CODE_VALUE, SCALE_VALUE = values_of_codes(), 2.0 ** (np.arange(256) - 127.0)
def decode(q):
    return (CODE_VALUE[q[0]].reshape(16, 8, -1, 4) * SCALE_VALUE[q[1]][:, None, :, None] + 0.0).reshape(128, -1).astype(np.float32)
def f(rng, *shape):
    return mx_ref.flush((rng.standard_normal(shape, dtype=np.float32) * np.exp2(rng.integers(-2, 3, shape[:-1] + (1,)))).astype(BF))
def wide(rng, *shape, cols=0):
    v = rng.standard_normal(shape, dtype=np.float32) * np.exp2(rng.integers(-12, 13, shape)).astype(np.float32)
    if cols: v *= np.repeat(np.exp2(rng.integers(-cols, cols + 1, shape[:-2] + (1, shape[-1] // 4))) * (rng.random(shape[:-2] + (1, shape[-1] // 4)) > 0.0625), 4, axis=-1).astype(np.float32)
    return mx_ref.flush(v.astype(BF))
C, A, R = 384, 320, 3
STEP = [1, 2, 4]
def nearest(s, a, b):
    at = lambda e: np.abs(s - np.take_along_axis(s, e, axis=1))
    return np.where(at(b) < at(a), b, a)
def depths(b):
    k = np.zeros((8, C), int)
    for i in range(1, C): k[:, i] = (k[np.arange(8), b[:, i]] + 1) % 4
    return k
def gput(t, e, h):
    a, b = t.reshape(8, 16, -1, 4).copy(), h.reshape(8, 16, -1, 4)
    for g in range(8): a[g][:, e[g]] = b[g]
    return a.reshape(128, -1)
def big(v):
    v = v.astype(np.float32)
    v[np.abs(v) < np.float32(2.0 ** -16)] = 0
    return v.astype(BF)
def numbers_of(rng):
    return {"x": big(f(rng, N, 128, 4 * C)), "u": np.array(f(rng, N, 128, 512)), "v": np.array(f(rng, N, 128, 512))}
def layers(rng):
    return big(f(rng, N, 128, 2048)).reshape(N, 8, 16, 4, 8, 16, 4)
def weights(rng, w):
    c, p = packed(np.ascontiguousarray(w).reshape(N, 128, 2048), rng)
    return {"wc": c, "ws": p}
def listed(a, b):
    return np.stack([gtable(np.concatenate([a[r], b[r]], axis=1)) for r in range(N)])
def candidates(rng):
    reach = np.stack([np.where(rng.permutation(8) < 4, C, 8) for r in range(N)])[:, :, None]
    n = np.minimum(np.maximum(np.arange(C), 1), reach)
    a, b = [np.maximum(np.arange(C) - 1 - rng.integers(0, n), 0) for k in range(2)]
    return {"cd": listed(a, b)}
def signs(rng):
    return np.stack([rng.permutation(8) % 2 * 2.0 - 1.0 for r in range(N)])
def setup_inputs(rng):
    return {**numbers_of(rng), **weights(rng, layers(rng)), **candidates(rng)}
def setup_inputs_ties(rng):
    d = numbers_of(rng)
    e = rng.permutation(N)
    x = d["x"].reshape(N, 8, 16, C, 4)
    for r in range(N):
        k = np.zeros(C, int) if r == e[0] else rng.permutation(C) % 3
        a = x[r][:, :8, :3].copy()
        a[:, :, 2] = 0
        x[r][:, :8] = a[:, :, k]
    x[e[1]] = 0
    u = d["u"].reshape(N, 8, 16, 128, 4)
    u[:, :, 8:, ::16] = 0
    w = layers(rng)
    w[:, :, :, :, :, :8] = 0
    return {"x": x.reshape(N, 128, 4 * C), "u": u.reshape(N, 128, 512), "v": d["v"], **weights(rng, w), **candidates(rng)}
def setup_inputs_near(rng):
    d = numbers_of(rng)
    x = np.zeros((N, 8, 16, C, 4), np.float32)
    u = d["u"].reshape(N, 128, 128, 4)
    u[:, :, ::16] = 0
    o, c = rng.permutation(N) % 4, signs(rng)
    for r in range(N):
        m = np.full((8, 1), 256)
        m[np.argsort(c[r], kind="stable")[::2]] = 4
        s = rng.integers(0, m, (8, C))
        size = 1.0 if o[r] < 2 else 2.0 ** -7
        g = ((s[:, :, None] >> np.arange(8)) & 1) * np.exp2(np.arange(8) - 23.0) * size
        if o[r] < 3: x[r, :, 0, :, 0] = c[r][:, None] * rng.integers(0, 2, (8, C)) * size
        x[r, :, 8] = g[:, :, :4]
        x[r, :, 9] = g[:, :, 4:]
        x[r, :, 10:] = rng.integers(4, 8, (8, 6, C, 4)) * 2.0 ** -22 * size
        k = 1.0 if o[r] == 0 else 2.0 ** -30
        for h in range(0, 128, 16):
            u[r, h, h, 0] = k
            u[r, h + 8:h + 10, h] = k
    w = layers(rng)
    w[:, :, :10] = 0
    w[:, :, :, :, :, :10] = 0
    return {"x": x.reshape(N, 128, 4 * C).astype(BF), "u": u.reshape(N, 128, 512), "v": d["v"], **weights(rng, w), **candidates(rng)}
def setup_inputs_huge(rng):
    d = numbers_of(rng)
    z = rng.permutation(N) < N // 2
    k = np.stack([rng.choice([-1.0, -0.25] if z[r] else [-1.0, -0.5, 0.5, 1.0], C) for r in range(N)])
    x = 2.0 ** 28 * (0.8 + 0.2 * rng.random((N, 128, C, 4))) * k[:, None, :, None]
    u = d["u"].reshape(N, 128, 128, 4)
    a = 2.0 ** 30 * (1 - 0.25 * rng.random((N, 128, 8, 4))) * signs(rng)[:, None, :, None]
    u[:, :, ::16] = a.astype(np.float32).astype(BF)
    w = np.zeros((N, 128, 4, 128, 4), np.float32)
    i = np.arange(128)
    for b in range(4): w[:, i, b, i, b] = -1
    return {"x": x.astype(np.float32).reshape(N, 128, 4 * C).astype(BF), "u": u.reshape(N, 128, 512), "v": d["v"], **weights(rng, w.astype(BF)), **candidates(rng)}
def shape(rng, k):
    if k == 0: return np.maximum(np.arange(C) - 1, 0)
    if k == 1: return np.zeros(C, int)
    if k == 8:
        b = np.full(C, 1)
        b[:2] = 0
        return b
    if k == 9:
        n = A - 24
        b = np.full(C, 3)
        b[:4] = 0, 0, 1, 2
        b[n + 3:n + 11] = n - 5 + rng.permutation(8)
        b[n + 11:n + 19] = n + 3 + rng.permutation(8)
        b[n + 19:] = n + 11 + rng.integers(0, 8, C - n - 19)
        return b
    n = [C - 3, A, A - 1, A + 1, A - 2, 1][k - 2]
    b = rng.integers(0, 3, C) if k in (3, 4, 5) else np.full(C, 2)
    b[:4] = 0, 0, 1, 2
    b[4 + rng.permutation(C - 4)[:n - 1]] = 3
    return b
def setup_inputs_trees(rng):
    d = setup_inputs(rng)
    m = rng.permutation(10)
    b = np.stack([np.stack([shape(rng, k) for k in rng.permutation(np.delete(np.arange(10), [m[r], m[r - 1]]))]) for r in range(N)])
    d["cd"] = listed(b, b)
    return d
def setup_inputs_spread(rng):
    d = setup_inputs(rng)
    d["x"] = big(wide(rng, N, 128, 4 * C, cols=6))
    return d
def check_inputs(d):
    b = []
    for k in ("x", "u", "v"):
        a = np.abs(d[k].astype(np.float32))
        if not (np.isfinite(a).all() and ((a == 0) | (a >= 2.0 ** -30) & (a <= 2.0 ** 30)).all()): b.append("a value of " + k)
    none, least, most = [emit(mx_ref.quantize(np.full((128, 16), k, np.float32).astype(BF)))[1][0, 0] for k in (0.0, 2.0 ** -30, 2.0 ** 30)]
    for r in range(N):
        if ((d["wc"][r] == 0x7F) | (d["wc"][r] == 0xFF)).any(): b.append("wc: a code that is no number")
        s = mx_ref.live(d["ws"][r])
        if ((s != none) & ((s < least) | (s > most))).any(): b.append("ws: a scale out of range")
        e = gentries(d["cd"][r]).reshape(8, 2, C)
        if ((e < 0) | (e > np.maximum(np.arange(C) - 1, 0))).any(): b.append("cd: a candidate that isn't lower")
    return b
def reference(x, u, v, wc, ws, cd):
    qu = [mx_ref.quantize(u[r]) for r in range(N)]
    lay = [pk(wc[r], ws[r]) for r in range(N)]
    can = [gentries(cd[r]) for r in range(N)]
    now = [x[r] for r in range(N)]
    for t in range(R):
        held, took, depth, base, sent = [], [], [], [], []
        for r in range(N):
            q = mx_ref.quantize(now[r])
            b = nearest(mx_ref.matmul(qu[r], q)[::16], can[r][:, :C], can[r][:, C:])
            k = depths(b)
            o = np.argsort(k, axis=1, kind="stable")[:, :A]
            place = np.zeros((8, C), int)
            np.put_along_axis(place, o, np.arange(A)[None], axis=1)
            k, b = np.take_along_axis(k, o, axis=1), np.take_along_axis(b, o, axis=1)
            h = decode(q).astype(BF)
            p = gcols(h, o).astype(np.float32) - gcols(h, np.where(k > 0, b, -1)).astype(np.float32)
            sent.append(mx_ref.quantize(p.astype(BF)))
            held.append(h)
            took.append(o)
            depth.append(k)
            base.append(np.take_along_axis(place, b, axis=1))
        made = []
        for r in range(N):
            e = (r - STEP[t]) % N
            m = decode(sent[e]).astype(BF)
            for k in (1, 2, 3): m = (m.astype(np.float32) + gcols(m, np.where(depth[e] == k, base[e], -1)).astype(np.float32)).astype(BF)
            q = mx_ref.quantize(m)
            z = gcols(held[r], took[r])
            h = tile([mx_ref.matmul(pick(lay[r], np.arange(128 * b, 128 * b + 128)), q) * np.float32(0.015625) + z[:, b::4].astype(np.float32) for b in range(4)])
            made.append(gput(held[r], took[r], h))
        now = made
    y = np.zeros((N, 128, C), np.float32)
    oc, osc = np.zeros((N, 128, 4 * C), np.uint8), np.zeros((N, 16, C), np.uint8)
    for r in range(N):
        q = mx_ref.quantize(now[r])
        y[r] = mx_ref.matmul(mx_ref.quantize(v[r]), q)
        oc[r], osc[r] = emit(q)
    return {"y": y, "oc": oc, "osc": osc}

@@ -1,0 +1,407 @@
+from concourse.mybir import dt, AluOpType, ActivationFunctionType
+
+C, A, R, N = 384, 320, 3, 8
+STEP = [1, 2, 4]
+Q, M = 24, 16
+PW = 400
+RW = 336
+YW = 528
+UNIT = 0.0009765625
+F4, U8 = "float8_e4m3fn_x4", "uint8"
+
+LISTS = [("lnat", 24, [[1, 24]], 0, 24),
+         ("lu", 8, [[16, 8]], 0, 0), ("ltot", 8, [[32, 4], [0, 2]], 31, 0),
+         ("ldup", 16, [[32, 4], [0, 2], [16, 2]], 0, 1), ("lcls", 8, [[0, 4], [16, 2]], 0, 1),
+         ("an", 48, [[256, 24], [0, 2]], 0, 6144), ("al", 24, [[2736, 24]], 0, 171),
+         ("bn", 48, [[48, 24], [24, 2]], 0, 1152), ("bl", 24, [[256, 24]], 0, 16),
+         ("ep", 48, [[32, 12], [1000, 2], [0, 2]], -1000, 1)]
+LAT, _a = {}, 0
+for _s, _n, _p, _b, _k in LISTS:
+    LAT[_s] = (_a, _a + _n)
+    _a += _n
+LW, LU = _a, LAT["an"][0]
+
+WIDTHS = {
+    "bfloat16": {"xt0": 4 * C, "ut": 512, "vt": 512, "one": 512, "onen": 512, "et": 2048, "en": 2048, "dg": 768, "rs": 1152, "rq": 128, "r5": 120,
+                 "mk": 256, "jid": C, "tb": 128, "tv": 128, "of": C, "og": A, "oh": A, "fp": 4 * PW, "fn": 4 * PW, "fo": 4 * PW,
+                 "pt": 4 * C, "ma": 4 * PW, "mb": 4 * PW, "mc": 4 * PW, "mg": 4 * PW, "md": 4 * PW, "mt": 4 * A, "xt": 4 * C},
+    "float32": {"zero": 16, "w1": 256, "w2": 256, "tbl": 800, "i6": C, "cls": 128, "sb": PW, "c1": 1152, "c2": 1152, "e1": 480, "e2": C,
+                "own": 16 + C, "y1": YW, "d2": YW, "ind": 128, "inc": 128, "bs": 256, "pu": 120, "pv": 120, "rp": 4 * RW, "yo": C},
+    "int32": {"cdf": 768, "dw": 24, "dm": 32, "pi": 1, "pm": 3, "ia": 768, "jj": 32, "li": LW, "lj": LW, "lk": LW, "lv": 72, "lw": 72, "lx": 72, "co": 72,
+              "k1": 48, "k2": 48, "k3": 48, "ke": 48},
+    "uint16": {"lists": LU, "lcb": 72, "lc": 48, "lie": 48, "lb": 30, "lpl": 24, "lpx": 24},
+    F4: {"wq": 512, "uq": 128, "urq": 128, "vq": 128, "xq": C, "eq": 512, "nq": 512, "pq": C, "mq": A, "oq": C},
+    U8: {"wp": 512, "up": 128, "urp": 128, "vp": 128, "xp": C, "ep": 512, "npl": 512, "pz": C, "mp": A, "op": C},
+}
+SCRATCH = {n: ("sbuf", [128, w], k) for k, m in WIDTHS.items() for n, w in m.items()}
+PART, _a = {}, 0
+for _s, _n in {"fc": 3, "ja": 32, "jb": 32, "jc": 32, "fr": 1, "da": 48, "db": 48, "dc": 48, "se": 24, "sm": 96, "sx": 96, "gg": 24, "sel": 192,
+               "seld": 96, "kf": 48, "kg": 48, "ks": 48, "kt": 48, "ls": 24, "pos": 24, "ps_": 64, "pr": 128}.items():
+    PART[_s] = (_a, _a + _n)
+    _a += _n
+SCRATCH["small"] = ("sbuf", [128, _a], "float32")
+SCRATCH["psA"] = SCRATCH["psB"] = ("psum", [128, 2048], "float32")
+for _t in range(R + 1):
+    SCRATCH["tq%d" % _t] = ("sbuf", [128, C], F4)
+    SCRATCH["tp%d" % _t] = ("sbuf", [128, C], U8)
+SENT = [("tq", "aq", F4, C), ("tp", "ap", U8, C), ("ql", "al", "uint16", 24), ("qo", "ao", "uint16", 20)]
+for _t in range(R):
+    for _s, _d, _k, _n in SENT:
+        if _s[0] == "q": SCRATCH["%s%d" % (_s, _t)] = ("sbuf", [128, _n], _k)
+        SCRATCH["%s%d" % (_d, _t)] = ("sbuf", [128, _n], _k)
+NDMA = 12
+SEMAPHORES = ["cv", "cs", "ct", "cg"] + ["d%d" % k for k in range(NDMA)] + ["%s_%s%d" % (a, b[0][1], t) for a in ("r", "l") for b in SENT for t in range(R)]
+
+
+def rank_program(g, core, T, topo):
+    rank = T.rank_of(core)
+    if rank is None:
+        return
+    OP, AF = AluOpType, ActivationFunctionType
+    eng = {"v": g.vector, "s": g.scalar, "t": g.tensor, "g": g, "y": g.sync}
+    csem = {"v": "cv", "s": "cs", "t": "ct", "g": "cg"}
+    count = {}
+    known = {q: {} for q in eng}
+    known["far"] = {}
+    log = {}
+    serial = [0]
+
+    def apart(r, o):
+        if r[2] <= o[1] or o[2] <= r[1]: return True
+        return r[3] > 1 and r[3] == o[3] and (r[1] - o[1]) % r[3] != 0
+
+    def psum(r): return r[0] in ("psA", "psB")
+
+    def widen(r):
+        return (r[0], r[1] // 512 * 512, (r[2] + 511) // 512 * 512, 1) if psum(r) else r
+
+    def settle(q, reads, writes):
+        need = {}
+        for w, rs in ((False, reads), (True, writes)):
+            for r in rs:
+                for o in log.get(r[0], ()):
+                    if apart(widen(r), o["r"]): continue
+                    if not (w or o["w"]) and not (psum(r) and o["q"] != q): continue
+                    need[o["n"]] = o
+        for n in sorted(need, reverse=True):
+            o = need[n]
+            if known[q].get(o["sem"], 0) >= o["val"]: continue
+            eng[q].wait_ge(T.sem[o["sem"]], o["val"])
+            for k, v in list(o["clock"].items()) + [(o["sem"], o["val"])]:
+                known[q][k] = max(known[q].get(k, 0), v)
+
+    def note(q, reads, writes, sem, val):
+        serial[0] += 1
+        clock = dict(known[q])
+        for w, rs in ((False, reads), (True, writes)):
+            for r in rs:
+                r = widen(r)
+                old = log.get(r[0], [])
+                if w and r[3] == 1: old = [o for o in old if not (r[1] <= o["r"][1] and o["r"][2] <= r[2])]
+                log[r[0]] = old + [{"r": r, "w": w, "q": q, "sem": sem, "val": val, "clock": clock, "n": serial[0]}]
+
+    def run(q, call, reads, writes):
+        settle(q, reads, writes)
+        s = csem[q]
+        count[s] = count.get(s, 0) + 1
+        call().then_inc(T.sem[s], 1)
+        note(q, reads, writes, s, count[s])
+
+    def B(name, a=0, b=None, step=1):
+        x, y = PART.get(name, (0, 0))
+        return ("small", x + a, y if b is None else x + b, step) if y else (name, a, SCRATCH[name][1][1] if b is None else b, step)
+
+    def L(name, buf="lists"): return B(buf, LAT[name][0], LAT[name][1])
+
+    def ap(r):
+        return T[r[0]][:, r[1]:r[2]] if r[3] == 1 else T[r[0]][:, r[1]:r[2]:r[3]]
+
+    def ind(r, off): return ap(r).indirect(ap(off))
+    def sc(x): return ap(x) if isinstance(x, tuple) else x
+    def rd(*xs): return [x for x in xs if isinstance(x, tuple)]
+
+    def fill(out, c): run("v", lambda: g.vector.memset(ap(out), c), [], [out])
+    def copy(out, i): run("v", lambda: g.vector.tensor_copy(ap(out), ap(i)), [i], [out])
+    def copyi(out, i, off): run("v", lambda: g.vector.tensor_copy(ap(out), ind(i, off)), [i, off], [out])
+    def tt(out, a, b, op): run("v", lambda: g.vector.tensor_tensor(ap(out), ap(a), ap(b), op), [a, b], [out])
+    def tti(out, a, off, b, op): run("v", lambda: g.vector.tensor_tensor(ap(out), ind(a, off), ap(b), op), [a, off, b], [out])
+    def ts(out, a, s1, op, s2=None, op1=None):
+        if op1 is None: run("v", lambda: g.vector.tensor_scalar(ap(out), ap(a), sc(s1), None, op), [a] + rd(s1), [out])
+        else: run("v", lambda: g.vector.tensor_scalar(ap(out), ap(a), sc(s1), sc(s2), op, op1), [a] + rd(s1, s2), [out])
+    def scan(out, keep, a): run("v", lambda: g.vector.tensor_tensor_scan(ap(out), ap(keep), ap(a), 0.0, OP.mult, OP.add), [keep, a], [out])
+    def quant(q, p, i): run("v", lambda: g.vector.quantize_mx(ap(q), ap(p), ap(i)), [i], [q, p])
+    def mm(out, a, asc, b, bsc): run("t", lambda: g.tensor.matmul_mx(ap(out), ap(a), ap(asc), ap(b), ap(bsc), True, True), [a, asc, b, bsc], [out])
+    def act(out, i): run("s", lambda: g.scalar.activation(ap(out), ap(i), AF.Copy), [i], [out])
+    def actm(out, i, k): run("s", lambda: g.scalar.activation(ap(out), ap(i), AF.Copy, scale=k), [i], [out])
+    def acta(out, i, k): run("s", lambda: g.scalar.activation(ap(out), ap(i), AF.Identity, bias=k), [i], [out])
+    def acti(out, i, off): run("s", lambda: g.scalar.activation(ap(out), ind(i, off), AF.Copy), [i, off], [out])
+    def pick(q, p, i, ip, off):
+        run("v", lambda: g.vector.tensor_copy(ap(q).bitcast(dt.uint32), ap(i).bitcast(dt.uint32).indirect(ap(off))), [i, off], [q])
+        acti(p, ip, off)
+    def iota(out, pattern, base, cm): run("g", lambda: g.iota(ap(out), pattern, base, cm), [], [out])
+    def iotaf(out, pattern, base, cm): run("g", lambda: g.iota(ap(out), pattern, base, cm, allow_small_or_imprecise_dtypes=True), [], [out])
+    def keep(out, i, pattern, op, base, cm): run("g", lambda: g.affine_select(ap(out), ap(i), pattern, op, 0.0, base, cm), [i], [out])
+    def units(name, ones):
+        for b in range(4): keep(B(name, 512 * b, 512 * b + 512), B(ones), [[1, 512]], OP.is_equal, -b, -4)
+    ndma = [0]
+
+    def dma(pairs, reads, writes):
+        s = "d%d" % ndma[0]
+        ndma[0] += 1
+        for q in sorted({p[0] for p in pairs}): settle(q, reads, writes)
+        for q, o, i in pairs: eng[q].dma_start(o, i).then_inc(T.sem[s], 16)
+        count[s] = 16 * len(pairs)
+        note(pairs[0][0], reads, writes, s, count[s])
+
+    def send(k, t):
+        s, d, kind, n = SENT[k]
+        dst, src = T.cores[(rank + STEP[t]) % N], "%s%d" % (s, t)
+        settle("g", [B(src)], [])
+        i, o = T[src][:, :], T["%s%d" % (d, t)][:, :]
+        if kind == F4: i, o = i.bitcast(dt.uint8), o.bitcast(dt.uint8)
+        ls, to = "l_%s%d" % (s[1], t), topo.addr(dst)
+        g.remote_dma(o, i, T.sem["r_%s%d" % (s[1], t)], T.sem[ls], to[1], to[0], topo.mask(core, dst))
+        count[ls] = len(topo.engines(core, dst))
+
+    def expect(k, t):
+        s, d, kind, n = SENT[k]
+        rs = "r_%s%d" % (s[1], t)
+        count[rs] = len(topo.engines(T.cores[(rank - STEP[t]) % N], core))
+        note("far", [], [B("%s%d" % (d, t))], rs, count[rs])
+
+    def plane(name, b): return B(name, PW * b, PW * b + PW)
+    def body(name, b): return B(name, PW * b, PW * b + C)
+    def side(name, b): return B(name, 128 * b, 128 * b + 128)
+
+    dma([("y", T.xt0[:, :], T.x[:, :])], [], [B("xt0")])
+    dma([("s", T.ut[:, :], T.u[:, :])], [], [B("ut")])
+    dma([("ys"[k % 2], T.cdf[k:128:16, :], T.cd[:, :]) for k in range(16)], [], [B("cdf")])
+    settle("y", [B("xt0")], [])
+    settle("s", [B("ut"), B("cdf")], [])
+    dma([("y", T.wq[:, :].bitcast(dt.uint8), T.wc[:, :])], [], [B("wq")])
+    dma([("s", T.wp[:, :], T.ws[:, :])], [], [B("wp")])
+    dma([("s", T.vt[:, :], T.v[:, :])], [], [B("vt")])
+
+    iota(B("pi"), [[0, 1]], 0, 1)
+    a = 0
+    while a < len(LISTS):
+        e = a
+        while e < len(LISTS) and LISTS[e][4] == LISTS[a][4]: e += 1
+        fill(B("lj", LAT[LISTS[a][0]][0], LAT[LISTS[e - 1][0]][1]), LISTS[a][4])
+        a = e
+    for s, n, p, b, k in LISTS: iota(L(s, "li"), p, b, 0)
+    fill(B("co", 0, 48), -767)
+    fill(B("co", 48, 72), -383)
+    iota(B("ia"), [[0, 48], [1, 16]], 128, -1)
+    fill(B("one"), 1.0)
+    for k in range(3): keep(B("rs", 384 * k, 384 * k + 384), B("one", 0, 384), [[0, 24], [1, 16]], OP.not_equal, 0, 0)
+    for k, n in ((0, 15), (1, 31), (2, 16)): ts(B("pm", k, k + 1), B("pi"), n, OP.bitwise_and)
+    copy(B("fc"), B("pm"))
+    pm, pr, po = B("fc", 0, 1), B("fc", 1, 2), B("fc", 2, 3)
+    ts(B("lk"), B("lj"), pm, OP.mult)
+    tt(B("lk"), B("lk"), B("li"), OP.add)
+    copy(B("lists"), B("lk", 0, LU))
+    x = LAT["an"][0]
+    ts(B("lv"), B("lk", x, x + 72), 12, OP.arith_shift_right)
+    quant(B("uq"), B("up"), B("ut"))
+    tt(B("lw"), B("lv"), B("co"), OP.mult)
+    pick(B("urq"), B("urp"), B("uq"), B("up"), L("lu"))
+    tt(B("lx"), B("lw"), B("lk", x + 72, x + 144), OP.add)
+    ts(B("ia"), B("ia"), 15, OP.bitwise_and)
+    copy(B("lcb"), B("lx"))
+    ts(B("dg"), B("ia"), 0.0, OP.is_equal)
+    units("et", "one")
+    fill(B("sb", C, PW), 0.0)
+    fill(B("onen"), -1.0)
+    fill(B("zero"), 0.0)
+
+    def lists_of_candidates():
+        tti(B("c1", 0, 768), B("cdf"), B("lcb", 0, 48), B("dg"), OP.mult)
+        scan(B("c2", 0, 768), B("rs", 0, 768), B("c1", 0, 768))
+        ts(B("k1"), B("c2", 15, 768, 16), 171.0, OP.mult)
+        ts(B("k3"), B("c2", 15, 768, 16), 16.0, OP.mult)
+        ts(B("k2"), B("k1"), 12, OP.arith_shift_right)
+        ts(B("fr"), pm, 0.0, OP.is_equal, 385.0, OP.mult)
+        ts(B("k2"), B("k2"), -383.0, OP.mult)
+        tt(B("ke"), B("k2"), B("k3"), OP.add)
+        ts(B("ke", 0, 2), B("ke", 0, 2), B("fr"), OP.add)
+        copy(B("lc"), B("ke"))
+
+    def lists_inside():
+        ts(B("k2"), B("ke"), 15, OP.bitwise_and)
+        tt(B("sel", 96, 144), B("ke"), L("ep", "lk"), OP.is_equal)
+        ts(B("kt"), B("ke"), -1.0, OP.mult, 386.0, OP.add)
+        ts(B("kf"), B("k2"), pm, OP.is_equal)
+        ts(B("k3"), B("ke"), 16.0, OP.add)
+        tt(B("kg"), B("kf"), B("sel", 96, 144), OP.subtract)
+        tt(B("kt"), B("kt"), B("kf"), OP.mult)
+        ts(B("ks"), B("sel", 96, 144), 14.0, OP.mult)
+        tt(B("sel", 0, 48), B("kg"), B("k3"), OP.mult)
+        tt(B("kt"), B("kt"), B("ke"), OP.add)
+        ts(B("sel", 144, 192), B("ke"), -float(C), OP.add)
+        tt(B("sel", 48, 96), B("kt"), B("ks"), OP.add)
+        tt(B("seld"), B("sel", 1, 192, 2), B("sel", 0, 192, 2), OP.subtract)
+
+    def table():
+        iotaf(B("i6"), [[1, 24], [32, 16]], 16, 0)
+        fill(B("tbl", C, 400), 0.0)
+        fill(B("tbl", 386, 387), UNIT)
+        acta(B("tbl", 0, C), B("i6"), UNIT)
+        acta(B("tbl", 400, 800), B("tbl", 0, 400), UNIT)
+        iota(B("jj"), [[1, 32]], 0, 0)
+        iotaf(B("jid"), [[1, C]], -192, 0)
+        keep(B("rq"), B("one", 0, 128), [[0, 4], [1, 32]], OP.not_equal, 0, 0)
+        keep(B("r5"), B("one", 0, 120), [[0, 24], [1, 5]], OP.not_equal, 0, 0)
+        iotaf(B("cls"), [[1, 4], [0, 32]], 0, 0)
+        units("en", "onen")
+
+    def late_constants():
+        fill(B("own", 0, 16), 0.0)
+        fill(B("y1", 0, 16), 0.0)
+        fill(B("y1", 400, YW), 0.0)
+        fill(B("e1"), 0.0)
+        for b in range(4):
+            for name in ("fn", "ma", "mb", "mc"): act(B(name, PW * b + C, PW * b + PW), B("zero"))
+            act(B("rp", RW * b + A, RW * b + RW), B("zero"))
+        return [lambda: fill(B("d2", 0, 16), 0.0), lambda: fill(B("dm"), 9.0), lambda: fill(B("w2"), 1.0),
+                lambda: ts(B("ja"), B("jj"), po, OP.subtract, 0.0, OP.is_ge),
+                lambda: ts(B("jb"), B("jj"), pr, OP.subtract, 0.0, OP.is_ge),
+                lambda: ts(B("jc"), B("jj"), po, OP.subtract, 16.0, OP.is_ge),
+                lambda: tt(B("mk", 0, 32), B("ja"), B("jb"), OP.subtract),
+                lambda: tt(B("mk", 32, 64), B("jb"), B("jc"), OP.subtract),
+                lambda: copy(B("mk", 64, 128), B("mk", 0, 64)),
+                lambda: copy(B("mk", 128, 256), B("mk", 0, 128)),
+                lambda: quant(B("nq"), B("npl"), B("en"))]
+
+    def leave(k):
+        for q in (k // 16, k // 16 + 1): ts(B("e1", q, 480, 32), B("y1", 17 + 16 * q, 32 + 16 * q), B("dg", q % 16, q % 16 + 1), OP.mult)
+
+    def settled(m):
+        ts(B("e2", m, C, 16), B("d2", 16 + 32 * m, 40 + 32 * m), B("dg", m, m + 1), OP.mult)
+
+    for t in range(R):
+        tq, tp, aq, apl, al, ao = ["%s%d" % (s, t) for s in ("tq", "tp", "aq", "ap", "al", "ao")]
+        if t == 0:
+            quant(B("xq"), B("xp"), B("xt0"))
+            pick(B(tq), B(tp), B("xq"), B("xp"), L("lnat"))
+        else:
+            for h in (0, 192): quant(B(tq, h, h + 192), B(tp, h, h + 192), B("xt", 4 * h, 4 * h + 768))
+        for h, k in ((0, 0), (192, 512)):
+            mm(B("psA", k, k + 192), B("urq"), B("urp"), B(tq, h, h + 192), B(tp, h, h + 192))
+            act(B("sb", h, h + 192), B("psA", k, k + 192))
+        send(0, t)
+        send(1, t)
+        if t == 0:
+            lists_of_candidates()
+            table()
+        tt(B("c1", 768, 960), B("psA", 0, 192), B("dg", 0, 192), OP.mult)
+        tti(B("c1", 0, 768), B("sb"), B("lc"), B("dg"), OP.mult)
+        tt(B("c1", 960, 1152), B("psA", 512, 704), B("dg", 0, 192), OP.mult)
+        scan(B("c2"), B("rs"), B("c1"))
+        if t == 0: lists_inside()
+        for h in (0, 1): tt(B("da", 24 * h, 24 * h + 24), B("c2", 16 * h + 15, 768, 32), B("c2", 783, 1152, 16), OP.subtract)
+        for h in (0, 1): tt(B("db", 24 * h, 24 * h + 24), B("c2", 783, 1152, 16), B("c2", 16 * h + 15, 768, 32), OP.subtract)
+        tt(B("dc"), B("da"), B("db"), OP.max)
+        tt(B("se"), B("dc", 24, 48), B("dc", 0, 24), OP.is_lt)
+        for h in (0, 24, 48): tt(B("sm", h, h + 24), B("seld", h, h + 24), B("se"), OP.mult)
+        tt(B("sx", 0, 72), B("sm", 0, 72), B("sel", 0, 144, 2), OP.add)
+        tt(B("sm", 72, 96), B("seld", 72, 96), B("se"), OP.mult)
+        for h in (0, 12): tt(B("gg", h, h + 12), B("sx", 49, 72, 2), B("sx", 2 * h, 2 * h + 24, 2), OP.mult)
+        tt(B("sx", 72, 96), B("sm", 72, 96), B("sel", 144, 192, 2), OP.add)
+        tt(B("sx", 1, 48, 2), B("sx", 1, 48, 2), B("gg"), OP.add)
+        copy(B("lie"), B("sx", 0, 48))
+        spare = late_constants() if t == 0 else []
+        if t == 0: quant(B("eq"), B("ep"), B("et"))
+        for x, y in ((0, 4), (4, 10), (10, 24)): acti(B("own", 16 + 16 * x, 16 + 16 * y), B("tbl"), B("lie", 24 + x, 24 + y))
+        for b in range(4):
+            mm(B("psB", 512 * b, 512 * b + C), side("eq", b), side("ep", b), B(tq), B(tp))
+            act(body("fp", b), B("psB", 512 * b, 512 * b + C))
+        for k in range(32, C, 32):
+            tti(B("y1", 16 + k, 48 + k), B("own" if k == 32 else "y1", 0, 16 + k), B("lie", k // 16, k // 16 + 2), B("own", 16 + k, 48 + k), OP.add)
+            if k == 32: copy(B("y1", 16, 48), B("own", 16, 48))
+            else: leave(k - 64)
+            for f in spare[:2]: f()
+            spare = spare[2:]
+        leave(C - 64)
+        leave(C - 32)
+        scan(B("c2", 0, 480), B("rs", 0, 480), B("e1"))
+        copy(B("d2", 16, 48), B("y1", 16, YW, 16))
+        copy(B("lb"), B("c2", 15, 480, 16))
+        for m in range(1, M):
+            tti(B("d2", 16 + 32 * m, 48 + 32 * m), B("d2", 0, 16 + 32 * m), B("lb", 2 * m - 2, 2 * m), B("y1", 16 + m, YW, 16), OP.add)
+            settled(m - 1)
+            for f in spare[:1]: f()
+            spare = spare[1:]
+        settled(M - 1)
+        scan(B("c2", 0, C), B("rs", 0, C), B("e2"))
+        ts(B("dw"), B("c2", 15, C, 16), 1 / UNIT, OP.mult)
+        ts(B("dm", 0, 24), B("dw"), 3, OP.bitwise_and)
+        ts(B("pos"), B("dm", 0, 24), 0.0, OP.is_gt)
+        tti(B("ind"), B("dm"), L("lcls"), B("cls"), OP.is_equal)
+        tt(B("ls"), B("sx", 72, 96), B("pos"), OP.mult)
+        scan(B("inc"), B("rq"), B("ind"))
+        ts(B("ql%d" % t), B("ls"), float(C), OP.add)
+        send(2, t)
+        copyi(B("tb"), B("inc"), L("ltot"))
+        tt(B("pr"), B("ind"), B("inc"), OP.mult)
+        run("v", lambda: g.vector.transpose(ap(B("tv")), ap(B("tb"))), [B("tb")], [B("tv")])
+        tt(B("ps_"), B("pr", 0, 64), B("pr", 64, 128), OP.add)
+        tti(B("w1"), B("tv"), L("ldup"), B("mk"), OP.mult)
+        tt(B("pu", 4, 120, 5), B("ps_", 0, 24), B("ps_", 32, 56), OP.add)
+        scan(B("bs"), B("w2"), B("w1"))
+        for c in range(4): ts(B("pu", c, 120, 5), B("ind", 32 * c, 32 * c + 24), B("bs", 64 * c + 31, 64 * c + 32), OP.mult)
+        scan(B("pv"), B("r5"), B("pu"))
+        ts(B("lpl"), B("pv", 4, 120, 5), -1.0, OP.add)
+        ts(B("lpx"), B("pv", 4, 120, 5), -1.0, OP.add, float(A), OP.min)
+        for k in range(4): expect(k, t)
+        for b in range(4):
+            mm(B("psA", 512 * b, 512 * b + C), side("nq", b), side("npl", b), B(aq), B(apl))
+            for name in ("fn", "fo")[:1 + (b < 2)]: act(body(name, b), B("psA", 512 * b, 512 * b + C))
+        for b in (2, 3): acti(body("mg", b), plane("fn", b), B(al))
+        for b in (0, 1): tti(B("pt", b, 4 * C, 4), plane("fn", b), B(al), body("fo", b), OP.subtract)
+        for b in (2, 3): tt(B("pt", b, 4 * C, 4), body("mg", b), B("psA", 512 * b, 512 * b + C), OP.subtract)
+        for h, ps in ((0, "psB"), (192, "psA")):
+            quant(B("pq", h, h + 192), B("pz", h, h + 192), B("pt", 4 * h, 4 * h + 768))
+            mm(B(ps, 0, 192), side("eq", 0), side("ep", 0), B("pq", h, h + 192), B("pz", h, h + 192))
+            act(B("ma", h, h + 192), B(ps, 0, 192))
+        for b in range(1, 4):
+            mm(B("psB", 512 * b, 512 * b + C), side("eq", b), side("ep", b), B("pq"), B("pz"))
+            act(body("ma", b), B("psB", 512 * b, 512 * b + C))
+            if b > 1: acti(body("mg", b), plane("ma", b), B(al))
+        run("v", lambda: g.vector.tensor_copy(ind(B("of"), B("lpl")), ap(B("jid"))), [B("jid"), B("lpl")], [B("of")])
+        order = [lambda: tt(B("og"), B("of", 0, A), B("dg", 0, A), OP.mult), lambda: scan(B("oh"), B("rs", 0, A), B("og")),
+                 lambda: ts(B("qo%d" % t), B("oh", 15, A, 16), 192.0, OP.add)]
+        for src, dst in (("ma", "mb"), ("mb", "mc"), ("mc", "mb")):
+            if src != "ma":
+                for b in (2, 3): acti(body("mg", b), plane(src, b), B(al))
+            for b in (0, 1):
+                if src == "ma":
+                    order[b]()
+                    copy(body("md", b), body("ma", b))
+                tti(body(dst, b), plane(src, b), B(al), body("md", b), OP.add)
+            if src == "ma":
+                order[2]()
+                send(3, t)
+            for b in (2, 3): tt(body(dst, b), body("mg", b), B("psB", 512 * b, 512 * b + C), OP.add)
+        for b in range(3): acti(B("mt", b, 4 * A, 4), plane("mb", b), B(ao))
+        acti(B("mt", 3, 640, 4), plane("mb", 3), B(ao, 0, 10))
+        copyi(B("mt", 643, 1280, 4), plane("mb", 3), B(ao, 10, 20))
+        for h, ps in ((0, "psA"), (160, "psB")):
+            quant(B("mq", h, h + 160), B("mp", h, h + 160), B("mt", 4 * h, 4 * h + 640))
+            mm(B(ps, 0, 160), side("wq", 0), side("wp", 0), B("mq", h, h + 160), B("mp", h, h + 160))
+            actm(B("rp", h, h + 160), B(ps, 0, 160), 0.015625)
+        if t == R - 1: quant(B("vq"), B("vp"), B("vt"))
+        for b in range(1, 4):
+            mm(B("psA", 512 * b, 512 * b + A), side("wq", b), side("wp", b), B("mq"), B("mp"))
+            actm(B("rp", RW * b, RW * b + A), B("psA", 512 * b, 512 * b + A), 0.015625)
+        for b in range(4):
+            tti(B("xt", b, 4 * C, 4), B("rp", RW * b, RW * b + RW), B("lpx"), body("fp", b), OP.add)
+
+    quant(B("tq%d" % R), B("tp%d" % R), B("xt"))
+    pick(B("oq"), B("op"), B("tq%d" % R), B("tp%d" % R), B("lcb", 48, 72))
+    dma([("y", T.oc[:, :], T.oq[:, :].bitcast(dt.uint8))], [B("oq")], [])
+    dma([("s", T.osc[4 * k:4 * k + 4, :], T.op[32 * k:32 * k + 4, :]) for k in range(4)], [B("op")], [])
+    mm(B("psB", 0, C), B("vq"), B("vp"), B("oq"), B("op"))
+    copy(B("yo"), B("psB", 0, C))
+    dma([("y", T.y[:, :], T.yo[:, :])], [B("yo")], [])
+    for s in sorted(count): g.wait_ge(T.sem[s], count[s])

@@ -3,40 +3,38 @@ from concourse.mybir import dt, AluOpType, ActivationFunctionType
 C, A, R, N = 384, 320, 3, 8
 STEP = [1, 2, 4]
 Q, M = 24, 16
-PW = 400
 RW = 336
 YW = 528
 UNIT = 0.0009765625
 F4, U8 = "float8_e4m3fn_x4", "uint8"
+WHOLE = [(), (), ()]
+WAIT = [12, 0, 3, 0, 0]
 
-LISTS = [("lnat", 24, [[1, 24]], 0, 24),
-         ("lu", 8, [[16, 8]], 0, 0), ("ltot", 8, [[32, 4], [0, 2]], 31, 0),
-         ("ldup", 16, [[32, 4], [0, 2], [16, 2]], 0, 1), ("lcls", 8, [[0, 4], [16, 2]], 0, 1),
-         ("an", 48, [[256, 24], [0, 2]], 0, 6144), ("al", 24, [[2736, 24]], 0, 171),
-         ("bn", 48, [[48, 24], [24, 2]], 0, 1152), ("bl", 24, [[256, 24]], 0, 16),
-         ("ep", 48, [[32, 12], [1000, 2], [0, 2]], -1000, 1)]
+PATTERNS = [("lu", 16, [[16, 2], [32, 4], [0, 2]], 0), ("lnat", 24, [[1, 24]], 0), ("lrun", 8, [[24, 2], [1, 2], [0, 2]], 0),
+            ("lpair", 4, [[32, 2], [8, 2]], 0), ("lown", 24, [[32, 12], [C, 2]], 0), ("first", 48, [[32, 12], [1000, 2], [0, 2]], -1000)]
 LAT, _a = {}, 0
-for _s, _n, _p, _b, _k in LISTS:
+for _s, _n, _p, _b in PATTERNS:
     LAT[_s] = (_a, _a + _n)
     _a += _n
-LW, LU = _a, LAT["an"][0]
+LW = _a
 
 WIDTHS = {
-    "bfloat16": {"xt0": 4 * C, "ut": 512, "vt": 512, "one": 512, "onen": 512, "et": 2048, "en": 2048, "dg": 768, "rs": 1152, "rq": 128, "r5": 120,
-                 "mk": 256, "jid": C, "tb": 128, "tv": 128, "of": C, "og": A, "oh": A, "fp": 4 * PW, "fn": 4 * PW, "fo": 4 * PW,
-                 "pt": 4 * C, "ma": 4 * PW, "mb": 4 * PW, "mc": 4 * PW, "mg": 4 * PW, "md": 4 * PW, "mt": 4 * A, "xt": 4 * C},
-    "float32": {"zero": 16, "w1": 256, "w2": 256, "tbl": 800, "i6": C, "cls": 128, "sb": PW, "c1": 1152, "c2": 1152, "e1": 480, "e2": C,
-                "own": 16 + C, "y1": YW, "d2": YW, "ind": 128, "inc": 128, "bs": 256, "pu": 120, "pv": 120, "rp": 4 * RW, "yo": C},
-    "int32": {"cdf": 768, "dw": 24, "dm": 32, "pi": 1, "pm": 3, "ia": 768, "jj": 32, "li": LW, "lj": LW, "lk": LW, "lv": 72, "lw": 72, "lx": 72, "co": 72,
-              "k1": 48, "k2": 48, "k3": 48, "ke": 48},
-    "uint16": {"lists": LU, "lcb": 72, "lc": 48, "lie": 48, "lb": 30, "lpl": 24, "lpx": 24},
-    F4: {"wq": 512, "uq": 128, "urq": 128, "vq": 128, "xq": C, "eq": 512, "nq": 512, "pq": C, "mq": A, "oq": C},
-    U8: {"wp": 512, "up": 128, "urp": 128, "vp": 128, "xp": C, "ep": 512, "npl": 512, "pz": C, "mp": A, "op": C},
+    "bfloat16": {"xt0": 4 * C, "ut": 512, "vt": 512, "one": 516, "et": 516, "ia": 480, "ib": A, "dg": A, "rs": 480, "rq": 128, "r5": 120,
+                 "hp": 128, "mk": 128, "fp": 4 * C, "fn": 4 * C, "ft": 4 * C,
+                 "pt": 4 * C, "gm": 16 * C, "mg": 8 * C, "md": 4 * C, "mt": 4 * A, "xt": 4 * C},
+    "float32": {"jt": 4 * C, "jv": C, "of": C, "og": A, "oh": A, "zero": 16, "tbl": 800, "i6": C, "sb": 2 * C, "c1": 1152, "c2": 1152, "e1": 480, "e2": C, "cb": 72, "b1": 128, "b2": 128,
+                "y1": YW, "d2": YW, "ind": 128, "inc": 128, "tv": 128, "w1": 132, "bs": 128, "tw": 128, "pu": 120, "pv": 120, "rp": 4 * RW,
+                "rg": C, "yo": C},
+    "int32": {"ca": 72, "dw": 24, "dm": 32, "pi": 1, "pm": 3, "li": LW, "k1": 72, "k2": 72, "k3": 72, "ke": 48},
+    "uint16": {"lu": 16, "lnat": 24, "lrun": 8, "lpair": 8, "lsel": 2, "lback": 24, "lc": 72, "lie": 48, "lb": 30, "lpl": 24, "lpx": 24, "lv": 24},
+    F4: {"wq": 512, "uq": 128, "urq": 256, "vq": 128, "xq": C, "eq": 512, "fq": C, "pq": C, "mq": A, "oq": C},
+    U8: {"wp": 512, "up": 128, "urp": 256, "vp": 128, "xp": C, "ep": 512, "fz": C, "pz": C, "mp": A, "op": C},
 }
 SCRATCH = {n: ("sbuf", [128, w], k) for k, m in WIDTHS.items() for n, w in m.items()}
 PART, _a = {}, 0
-for _s, _n in {"fc": 3, "ja": 32, "jb": 32, "jc": 32, "fr": 1, "da": 48, "db": 48, "dc": 48, "se": 24, "sm": 96, "sx": 96, "gg": 24, "sel": 192,
-               "seld": 96, "kf": 48, "kg": 48, "ks": 48, "kt": 48, "ls": 24, "pos": 24, "ps_": 64, "pr": 128}.items():
+for _s, _n in {"fc": 3, "mh": 1, "t1": 1, "z1": 1, "t2": 1, "t3": 1, "t4": 1, "m24": 1, "up384": 1, "even": 1, "fr": 1, "fs": 48, "kb": 112, "kc": 112,
+               "kd": 112, "da": 48, "db": 48, "dc": 48, "se": 24, "sm": 96, "sx": 96, "gg": 24, "sel": 192, "seld": 96, "kf": 48, "kg": 48,
+               "ks": 48, "kt": 48, "ls": 24, "pos": 24, "ps_": 64, "pr": 128, "base": 16}.items():
     PART[_s] = (_a, _a + _n)
     _a += _n
 SCRATCH["small"] = ("sbuf", [128, _a], "float32")
@@ -68,7 +66,10 @@ def rank_program(g, core, T, topo):
 
     def apart(r, o):
         if r[2] <= o[1] or o[2] <= r[1]: return True
-        return r[3] > 1 and r[3] == o[3] and (r[1] - o[1]) % r[3] != 0
+        if r[3] > 1 and r[3] == o[3]: return (r[1] - o[1]) % r[3] != 0
+        for s, n in ((r, o), (o, r)):
+            if n[3] == 1 and s[3] > 1 and (s[1] - n[1]) % s[3] >= n[2] - n[1]: return True
+        return False
 
     def psum(r): return r[0] in ("psA", "psB")
 
@@ -111,7 +112,7 @@ def rank_program(g, core, T, topo):
         x, y = PART.get(name, (0, 0))
         return ("small", x + a, y if b is None else x + b, step) if y else (name, a, SCRATCH[name][1][1] if b is None else b, step)
 
-    def L(name, buf="lists"): return B(buf, LAT[name][0], LAT[name][1])
+    def L(name): return B("li", LAT[name][0], LAT[name][1])
 
     def ap(r):
         return T[r[0]][:, r[1]:r[2]] if r[3] == 1 else T[r[0]][:, r[1]:r[2]:r[3]]
@@ -129,11 +130,12 @@ def rank_program(g, core, T, topo):
         if op1 is None: run("v", lambda: g.vector.tensor_scalar(ap(out), ap(a), sc(s1), None, op), [a] + rd(s1), [out])
         else: run("v", lambda: g.vector.tensor_scalar(ap(out), ap(a), sc(s1), sc(s2), op, op1), [a] + rd(s1, s2), [out])
     def scan(out, keep, a): run("v", lambda: g.vector.tensor_tensor_scan(ap(out), ap(keep), ap(a), 0.0, OP.mult, OP.add), [keep, a], [out])
+    def turn(out, i): run("v", lambda: g.vector.transpose(ap(out), ap(i)), [i], [out])
     def quant(q, p, i): run("v", lambda: g.vector.quantize_mx(ap(q), ap(p), ap(i)), [i], [q, p])
     def mm(out, a, asc, b, bsc): run("t", lambda: g.tensor.matmul_mx(ap(out), ap(a), ap(asc), ap(b), ap(bsc), True, True), [a, asc, b, bsc], [out])
     def act(out, i): run("s", lambda: g.scalar.activation(ap(out), ap(i), AF.Copy), [i], [out])
     def actm(out, i, k): run("s", lambda: g.scalar.activation(ap(out), ap(i), AF.Copy, scale=k), [i], [out])
-    def acta(out, i, k): run("s", lambda: g.scalar.activation(ap(out), ap(i), AF.Identity, bias=k), [i], [out])
+    def actf(out, i, f, k, c): run("s", lambda: g.scalar.activation(ap(out), ap(i), f, bias=sc(c), scale=k), [i] + rd(c), [out])
     def acti(out, i, off): run("s", lambda: g.scalar.activation(ap(out), ind(i, off), AF.Copy), [i, off], [out])
     def pick(q, p, i, ip, off):
         run("v", lambda: g.vector.tensor_copy(ap(q).bitcast(dt.uint32), ap(i).bitcast(dt.uint32).indirect(ap(off))), [i, off], [q])
@@ -141,8 +143,6 @@ def rank_program(g, core, T, topo):
     def iota(out, pattern, base, cm): run("g", lambda: g.iota(ap(out), pattern, base, cm), [], [out])
     def iotaf(out, pattern, base, cm): run("g", lambda: g.iota(ap(out), pattern, base, cm, allow_small_or_imprecise_dtypes=True), [], [out])
     def keep(out, i, pattern, op, base, cm): run("g", lambda: g.affine_select(ap(out), ap(i), pattern, op, 0.0, base, cm), [i], [out])
-    def units(name, ones):
-        for b in range(4): keep(B(name, 512 * b, 512 * b + 512), B(ones), [[1, 512]], OP.is_equal, -b, -4)
     ndma = [0]
 
     def dma(pairs, reads, writes):
@@ -169,109 +169,100 @@ def rank_program(g, core, T, topo):
         count[rs] = len(topo.engines(T.cores[(rank - STEP[t]) % N], core))
         note("far", [], [B("%s%d" % (d, t))], rs, count[rs])
 
-    def plane(name, b): return B(name, PW * b, PW * b + PW)
-    def body(name, b): return B(name, PW * b, PW * b + C)
+    def body(name, b): return B(name, C * b, C * b + C)
     def side(name, b): return B(name, 128 * b, 128 * b + 128)
+    def bank(ps, b, n=C): return B(ps, 512 * b, 512 * b + n)
 
-    dma([("y", T.xt0[:, :], T.x[:, :])], [], [B("xt0")])
+    dma([("y", T.ca[:, 0:48], T.cd[:, :])], [], [B("ca", 0, 48)])
     dma([("s", T.ut[:, :], T.u[:, :])], [], [B("ut")])
-    dma([("ys"[k % 2], T.cdf[k:128:16, :], T.cd[:, :]) for k in range(16)], [], [B("cdf")])
+    dma([("y", T.xt0[:, :], T.x[:, :])], [], [B("xt0")])
     settle("y", [B("xt0")], [])
-    settle("s", [B("ut"), B("cdf")], [])
     dma([("y", T.wq[:, :].bitcast(dt.uint8), T.wc[:, :])], [], [B("wq")])
-    dma([("s", T.wp[:, :], T.ws[:, :])], [], [B("wp")])
-    dma([("s", T.vt[:, :], T.v[:, :])], [], [B("vt")])
+    dma([("y", T.wp[:, :], T.ws[:, :])], [], [B("wp")])
+    dma([("y", T.vt[:, :], T.v[:, :])], [], [B("vt")])
 
     iota(B("pi"), [[0, 1]], 0, 1)
-    a = 0
-    while a < len(LISTS):
-        e = a
-        while e < len(LISTS) and LISTS[e][4] == LISTS[a][4]: e += 1
-        fill(B("lj", LAT[LISTS[a][0]][0], LAT[LISTS[e - 1][0]][1]), LISTS[a][4])
-        a = e
-    for s, n, p, b, k in LISTS: iota(L(s, "li"), p, b, 0)
-    fill(B("co", 0, 48), -767)
-    fill(B("co", 48, 72), -383)
-    iota(B("ia"), [[0, 48], [1, 16]], 128, -1)
+    for s, n, p, b in PATTERNS: iota(L(s), p, b, 0)
     fill(B("one"), 1.0)
-    for k in range(3): keep(B("rs", 384 * k, 384 * k + 384), B("one", 0, 384), [[0, 24], [1, 16]], OP.not_equal, 0, 0)
-    for k, n in ((0, 15), (1, 31), (2, 16)): ts(B("pm", k, k + 1), B("pi"), n, OP.bitwise_and)
-    copy(B("fc"), B("pm"))
-    pm, pr, po = B("fc", 0, 1), B("fc", 1, 2), B("fc", 2, 3)
-    ts(B("lk"), B("lj"), pm, OP.mult)
-    tt(B("lk"), B("lk"), B("li"), OP.add)
-    copy(B("lists"), B("lk", 0, LU))
-    x = LAT["an"][0]
-    ts(B("lv"), B("lk", x, x + 72), 12, OP.arith_shift_right)
-    quant(B("uq"), B("up"), B("ut"))
-    tt(B("lw"), B("lv"), B("co"), OP.mult)
-    pick(B("urq"), B("urp"), B("uq"), B("up"), L("lu"))
-    tt(B("lx"), B("lw"), B("lk", x + 72, x + 144), OP.add)
-    ts(B("ia"), B("ia"), 15, OP.bitwise_and)
-    copy(B("lcb"), B("lx"))
-    ts(B("dg"), B("ia"), 0.0, OP.is_equal)
-    units("et", "one")
-    fill(B("sb", C, PW), 0.0)
-    fill(B("onen"), -1.0)
     fill(B("zero"), 0.0)
+    for k, n in enumerate((15, 16, 1)): ts(B("pm", k, k + 1), B("pi"), n, OP.bitwise_and)
+    copy(B("lu"), L("lu"))
+    copy(B("fc"), B("pm"))
+    pm, po, odd = B("fc", 0, 1), B("fc", 1, 2), B("fc", 2, 3)
+    mh, up = B("mh"), B("up384")
+    ts(mh, pm, odd, OP.subtract, 0.5, OP.mult)
+    ts(up, po, C / 16, OP.mult)
+    ts(B("ca", 48, 72), L("lnat"), 16.0, OP.mult, pm, OP.add)
+    ts(B("m24"), pm, float(Q), OP.mult)
+    ts(B("t1"), odd, 16.0, OP.mult, mh, OP.add)
+    ts(B("lrun"), L("lrun"), mh, OP.add, pm, OP.add)
+    ts(B("t2"), odd, 64.0, OP.mult, mh, OP.add)
+    ts(B("z1"), po, 4.0, OP.mult, B("t1"), OP.add)
+    ts(B("lnat"), L("lnat"), B("m24"), OP.add)
+    ts(B("lpair", 4, 8), L("lpair"), B("t2"), OP.add, po, OP.add)
+    ts(B("lpair", 0, 4), L("lpair"), B("z1"), OP.add)
+    ts(B("even"), odd, -1.0, OP.mult, 1.0, OP.add)
+    ts(B("lc", 48, 72), L("lown"), pm, OP.add, po, OP.add)
+    keep(B("et"), B("one"), [[1, 516]], OP.is_equal, -3, -4)
+    iotaf(B("i6"), [[1, 24], [32, 16]], 16, 0)
+    iotaf(B("ia"), [[0, 30], [1, 16]], 0, 0)
+
+    ts(B("k1"), B("ca"), 1 / Q, OP.mult, -0.479, OP.add)
+    ts(B("k3"), B("ca"), 16.0, OP.mult, up, OP.add)
+    ts(B("k2"), B("k1"), -383.0, OP.mult)
+    quant(B("uq"), B("up"), B("ut"))
+    tt(B("cb"), B("k2"), B("k3"), OP.add)
+    pick(B("urq"), B("urp"), B("uq"), B("up"), B("lu"))
+    copyi(B("b1"), B("cb", 0, 48), B("lrun"))
+    ts(B("fr"), pm, 0.0, OP.is_equal, 385.0, OP.mult)
+    for b in (0, 1): quant(side("eq", b), side("ep", b), B("et", 3 - b, 515 - b))
+    turn(B("b2"), B("b1"))
+    ts(B("fs"), L("first"), pm, OP.add)
+    for b in (2, 3): quant(side("eq", b), side("ep", b), B("et", 3 - b, 515 - b))
+    copyi(B("b1"), B("b2"), B("lpair"))
+    act(B("tbl", C, 400), B("zero"))
+    actf(B("tbl", 386, 387), B("zero", 0, 1), AF.Identity, 1.0, UNIT)
+    actf(B("tbl", 0, C), B("i6"), AF.Identity, 1.0, UNIT)
+    actf(B("tbl", 400, 800), B("tbl", 0, 400), AF.Identity, 1.0, UNIT)
+    act(B("y1", 0, 16), B("zero"))
+    quant(B("xq"), B("xp"), B("xt0"))
+    pick(B("tq0"), B("tp0"), B("xq"), B("xp"), B("lnat"))
 
     def lists_of_candidates():
-        tti(B("c1", 0, 768), B("cdf"), B("lcb", 0, 48), B("dg"), OP.mult)
-        scan(B("c2", 0, 768), B("rs", 0, 768), B("c1", 0, 768))
-        ts(B("k1"), B("c2", 15, 768, 16), 171.0, OP.mult)
-        ts(B("k3"), B("c2", 15, 768, 16), 16.0, OP.mult)
-        ts(B("k2"), B("k1"), 12, OP.arith_shift_right)
-        ts(B("fr"), pm, 0.0, OP.is_equal, 385.0, OP.mult)
-        ts(B("k2"), B("k2"), -383.0, OP.mult)
-        tt(B("ke"), B("k2"), B("k3"), OP.add)
+        ts(B("kb"), B("b1", 0, 112), B("even"), OP.mult)
+        ts(B("kc"), B("b1", 16, 128), odd, OP.mult)
+        tt(B("kd"), B("kb"), B("kc"), OP.add)
+        copy(B("lc", 0, 48), B("kd", 0, 48))
+        ts(B("ke"), B("kd", 64, 112), up, OP.subtract)
         ts(B("ke", 0, 2), B("ke", 0, 2), B("fr"), OP.add)
-        copy(B("lc"), B("ke"))
 
     def lists_inside():
-        ts(B("k2"), B("ke"), 15, OP.bitwise_and)
-        tt(B("sel", 96, 144), B("ke"), L("ep", "lk"), OP.is_equal)
-        ts(B("kt"), B("ke"), -1.0, OP.mult, 386.0, OP.add)
-        ts(B("kf"), B("k2"), pm, OP.is_equal)
-        ts(B("k3"), B("ke"), 16.0, OP.add)
-        tt(B("kg"), B("kf"), B("sel", 96, 144), OP.subtract)
-        tt(B("kt"), B("kt"), B("kf"), OP.mult)
-        ts(B("ks"), B("sel", 96, 144), 14.0, OP.mult)
-        tt(B("sel", 0, 48), B("kg"), B("k3"), OP.mult)
-        tt(B("kt"), B("kt"), B("ke"), OP.add)
-        ts(B("sel", 144, 192), B("ke"), -float(C), OP.add)
-        tt(B("sel", 48, 96), B("kt"), B("ks"), OP.add)
+        k2, k3 = B("k2", 0, 48), B("k3", 0, 48)
+        ts(k2, B("ke"), 15, OP.bitwise_and)
+        tt(B("sel", 96, 144), B("ke"), B("fs"), OP.is_equal)
+        ts(k3, B("ke"), 16.0, OP.add)
+        ts(B("kf"), k2, pm, OP.is_equal, 386.0, OP.mult)
+        ts(B("ks"), B("sel", 96, 144), 400.0, OP.mult)
+        tt(B("kt"), B("kf"), B("ke"), OP.max)
+        ts(B("sel", 144, 192), B("ke"), C - 1.0, OP.min)
+        tt(B("sel", 48, 96), B("kt"), B("ks"), OP.max)
+        ts(B("kg"), B("sel", 48, 96), 386.0, OP.is_equal, 1000.0, OP.mult)
+        tt(B("sel", 0, 48), B("kg"), k3, OP.min)
         tt(B("seld"), B("sel", 1, 192, 2), B("sel", 0, 192, 2), OP.subtract)
 
-    def table():
-        iotaf(B("i6"), [[1, 24], [32, 16]], 16, 0)
-        fill(B("tbl", C, 400), 0.0)
-        fill(B("tbl", 386, 387), UNIT)
-        acta(B("tbl", 0, C), B("i6"), UNIT)
-        acta(B("tbl", 400, 800), B("tbl", 0, 400), UNIT)
-        iota(B("jj"), [[1, 32]], 0, 0)
-        iotaf(B("jid"), [[1, C]], -192, 0)
+    def late_constants():
+        actf(B("ib"), B("ia", 0, A), AF.Abs, -1.0, pm)
+        actf(B("dg"), B("ib"), AF.Relu, -1.0, 1.0)
+        iotaf(B("hp"), [[0, 4], [1, 2], [0, 16]], 0, 0)
         keep(B("rq"), B("one", 0, 128), [[0, 4], [1, 32]], OP.not_equal, 0, 0)
         keep(B("r5"), B("one", 0, 120), [[0, 24], [1, 5]], OP.not_equal, 0, 0)
-        iotaf(B("cls"), [[1, 4], [0, 32]], 0, 0)
-        units("en", "onen")
-
-    def late_constants():
-        fill(B("own", 0, 16), 0.0)
-        fill(B("y1", 0, 16), 0.0)
-        fill(B("y1", 400, YW), 0.0)
-        fill(B("e1"), 0.0)
-        for b in range(4):
-            for name in ("fn", "ma", "mb", "mc"): act(B(name, PW * b + C, PW * b + PW), B("zero"))
-            act(B("rp", RW * b + A, RW * b + RW), B("zero"))
-        return [lambda: fill(B("d2", 0, 16), 0.0), lambda: fill(B("dm"), 9.0), lambda: fill(B("w2"), 1.0),
-                lambda: ts(B("ja"), B("jj"), po, OP.subtract, 0.0, OP.is_ge),
-                lambda: ts(B("jb"), B("jj"), pr, OP.subtract, 0.0, OP.is_ge),
-                lambda: ts(B("jc"), B("jj"), po, OP.subtract, 16.0, OP.is_ge),
-                lambda: tt(B("mk", 0, 32), B("ja"), B("jb"), OP.subtract),
-                lambda: tt(B("mk", 32, 64), B("jb"), B("jc"), OP.subtract),
-                lambda: copy(B("mk", 64, 128), B("mk", 0, 64)),
-                lambda: copy(B("mk", 128, 256), B("mk", 0, 128)),
-                lambda: quant(B("nq"), B("npl"), B("en"))]
+        actm(B("e1"), B("one", 0, 480), 0.0)
+        actm(B("y1", 400, YW), B("one", 0, YW - 400), 0.0)
+        act(B("d2", 0, 16), B("zero"))
+        actf(B("rs"), B("ia"), AF.Sign, 1.0, 0.0)
+        act(B("rp", A, 4 * RW, RW), B("zero", 0, 4))
+        act(B("w1", 0, 1), B("zero", 0, 1))
+        actf(B("mk"), B("hp"), AF.Abs, -1.0, odd)
 
     def leave(k):
         for q in (k // 16, k // 16 + 1): ts(B("e1", q, 480, 32), B("y1", 17 + 16 * q, 32 + 16 * q), B("dg", q % 16, q % 16 + 1), OP.mult)
@@ -279,28 +270,85 @@ def rank_program(g, core, T, topo):
     def settled(m):
         ts(B("e2", m, C, 16), B("d2", 16 + 32 * m, 40 + 32 * m), B("dg", m, m + 1), OP.mult)
 
+    def unpack(ps, q, p):
+        for b in range(4): mm(bank(ps, b), side("eq", b), side("ep", b), B(q), B(p))
+
+    jobs = []
+
+    def slot():
+        if jobs: jobs.pop(0)()
+
+    def rebuild(t):
+        aq, apl, al = "aq%d" % t, "ap%d" % t, "al%d" % t
+        def made(b, d, a=0, e=C): return B("gm", C * (4 * b + d) + a, C * (4 * b + d) + e)
+        def near(b, d, a=0, e=C): return B("mg", C * (4 * (d % 2) + b) + a, C * (4 * (d % 2) + b) + e)
+        def half(ps, b, h): return B(ps, 512 * b + h, 512 * b + h + 192)
+        def wait(n): jobs.extend([lambda: None] * n)
+
+        def columns():
+            for x in range(2): expect(x, t)
+            unpack("psA", aq, apl)
+            for b in range(4):
+                act(body("fn", b), bank("psA", b))
+                act(B("ft", b, 4 * C, 4), bank("psA", b))
+
+        def roots(h):
+            quant(B("fq", h, h + 192), B("fz", h, h + 192), B("ft", 4 * h, 4 * h + 768))
+            if h:
+                unpack("psB", "fq", "fz")
+                expect(2, t)
+                for b in range(4): acti(near(b, 0), body("fn", b), B(al))
+                for b in range(4): act(made(b, 0), bank("psB", b))
+                for b in range(4):
+                    if b not in WHOLE[0]: acti(near(b, 1), made(b, 0), B(al))
+
+        def pack(h):
+            quant(B("pq", h, h + 192), B("pz", h, h + 192), B("pt", 4 * h, 4 * h + 768))
+            if h:
+                unpack("psB", "pq", "pz")
+                for b in sorted(set(sum(WHOLE, ()))): act(body("md", b), bank("psB", b))
+
+        def step(d, b, h):
+            if b in WHOLE[d - 1]: tti(made(b, d, h, h + 192), made(b, d - 1), B(al, h // 16, h // 16 + 12), B("md", C * b + h, C * b + h + 192), OP.add)
+            else: tt(made(b, d, h, h + 192), near(b, d, h, h + 192), half("psB", b, h), OP.add)
+            if h and d < 3 and b not in WHOLE[d]: acti(near(b, d + 1), made(b, d), B(al))
+
+        columns()
+        if t == 0:
+            jobs.extend([lambda: fill(B("dm"), 9.0), lambda: ts(B("t3"), pm, 3.0, OP.min, 32.0, OP.mult),
+                         lambda: ts(B("t4"), po, -1 / 16, OP.mult, 31.0, OP.add), lambda: ts(B("lsel", 0, 1), B("t3"), B("t4"), OP.add),
+                         lambda: ts(B("lback"), B("cb", 48, 72), up, OP.subtract)])
+        wait(WAIT[0] - len(jobs))
+        jobs.extend([lambda h=h: roots(h) for h in (0, 192)])
+        wait(WAIT[1])
+        jobs.extend([lambda b=b, h=h: tt(B("pt", 4 * h + b, 4 * h + 768, 4), half("psA", b, h), near(b, 0, h, h + 192), OP.subtract)
+                     for b in range(4) for h in (0, 192)])
+        jobs.extend([lambda h=h: pack(h) for h in (0, 192)])
+        for d in (1, 2, 3):
+            wait(WAIT[d + 1])
+            jobs.extend([lambda d=d, b=b, h=h: step(d, b, h) for b in range(4) for h in (0, 192)])
+
     for t in range(R):
         tq, tp, aq, apl, al, ao = ["%s%d" % (s, t) for s in ("tq", "tp", "aq", "ap", "al", "ao")]
-        if t == 0:
-            quant(B("xq"), B("xp"), B("xt0"))
-            pick(B(tq), B(tp), B("xq"), B("xp"), L("lnat"))
-        else:
+        if t:
             for h in (0, 192): quant(B(tq, h, h + 192), B(tp, h, h + 192), B("xt", 4 * h, 4 * h + 768))
-        for h, k in ((0, 0), (192, 512)):
-            mm(B("psA", k, k + 192), B("urq"), B("urp"), B(tq, h, h + 192), B(tp, h, h + 192))
-            act(B("sb", h, h + 192), B("psA", k, k + 192))
+        for k in range(4):
+            h, o = 192 * (k // 2), k % 2
+            mm(bank("psA", k, 192), side("urq", o), side("urp", o), B(tq, h, h + 192), B(tp, h, h + 192))
+            if k < 3: act(B("sb", C * o + h, C * o + h + 192), bank("psA", k, 192))
         send(0, t)
         send(1, t)
-        if t == 0:
-            lists_of_candidates()
-            table()
-        tt(B("c1", 768, 960), B("psA", 0, 192), B("dg", 0, 192), OP.mult)
-        tti(B("c1", 0, 768), B("sb"), B("lc"), B("dg"), OP.mult)
-        tt(B("c1", 960, 1152), B("psA", 512, 704), B("dg", 0, 192), OP.mult)
-        scan(B("c2"), B("rs"), B("c1"))
+        if t == 0: lists_of_candidates()
+        copy(B("sb", C + 192, 2 * C), bank("psA", 3, 192))
         if t == 0: lists_inside()
-        for h in (0, 1): tt(B("da", 24 * h, 24 * h + 24), B("c2", 16 * h + 15, 768, 32), B("c2", 783, 1152, 16), OP.subtract)
-        for h in (0, 1): tt(B("db", 24 * h, 24 * h + 24), B("c2", 783, 1152, 16), B("c2", 16 * h + 15, 768, 32), OP.subtract)
+        for k in (1, 2): acti(B("c1", C * k, C * k + C), B("sb"), B("lc", Q * k, Q * k + Q))
+        copyi(B("c1", 0, C), B("sb"), B("lc", 0, Q))
+        if t == 0: late_constants()
+        unpack("psB", tq, tp)
+        for b in range(4): act(body("fp", b), bank("psB", b))
+        for k in range(3): turn(B("c2", C * k, C * k + C), B("c1", C * k, C * k + C))
+        for h in (0, 1): tt(B("da", 24 * h, 24 * h + 24), B("c2", 16 * h, 768, 32), B("c2", 768, 1152, 16), OP.subtract)
+        for h in (0, 1): tt(B("db", 24 * h, 24 * h + 24), B("c2", 768, 1152, 16), B("c2", 16 * h, 768, 32), OP.subtract)
         tt(B("dc"), B("da"), B("db"), OP.max)
         tt(B("se"), B("dc", 24, 48), B("dc", 0, 24), OP.is_lt)
         for h in (0, 24, 48): tt(B("sm", h, h + 24), B("seld", h, h + 24), B("se"), OP.mult)
@@ -309,99 +357,85 @@ def rank_program(g, core, T, topo):
         for h in (0, 12): tt(B("gg", h, h + 12), B("sx", 49, 72, 2), B("sx", 2 * h, 2 * h + 24, 2), OP.mult)
         tt(B("sx", 72, 96), B("sm", 72, 96), B("sel", 144, 192, 2), OP.add)
         tt(B("sx", 1, 48, 2), B("sx", 1, 48, 2), B("gg"), OP.add)
+        copy(B("ql%d" % t), B("sx", 72, 96))
+        send(2, t)
         copy(B("lie"), B("sx", 0, 48))
-        spare = late_constants() if t == 0 else []
-        if t == 0: quant(B("eq"), B("ep"), B("et"))
-        for x, y in ((0, 4), (4, 10), (10, 24)): acti(B("own", 16 + 16 * x, 16 + 16 * y), B("tbl"), B("lie", 24 + x, 24 + y))
-        for b in range(4):
-            mm(B("psB", 512 * b, 512 * b + C), side("eq", b), side("ep", b), B(tq), B(tp))
-            act(body("fp", b), B("psB", 512 * b, 512 * b + C))
+        copyi(B("y1", 16, 80), B("tbl"), B("lie", 24, 28))
+        for x, y in ((4, 10), (10, 24)): acti(B("y1", 16 + 16 * x, 16 + 16 * y), B("tbl"), B("lie", 24 + x, 24 + y))
+        if t == 0: iotaf(B("jt"), [[1, 4 * C]], 0, 0)
+        rebuild(t)
         for k in range(32, C, 32):
-            tti(B("y1", 16 + k, 48 + k), B("own" if k == 32 else "y1", 0, 16 + k), B("lie", k // 16, k // 16 + 2), B("own", 16 + k, 48 + k), OP.add)
-            if k == 32: copy(B("y1", 16, 48), B("own", 16, 48))
-            else: leave(k - 64)
-            for f in spare[:2]: f()
-            spare = spare[2:]
-        leave(C - 64)
+            tti(B("y1", 16 + k, 48 + k), B("y1", 0, 16 + k), B("lie", k // 16, k // 16 + 2), B("y1", 16 + k, 48 + k), OP.add)
+            leave(k - 32)
+            slot()
         leave(C - 32)
-        scan(B("c2", 0, 480), B("rs", 0, 480), B("e1"))
+        slot()
+        scan(B("c2", 0, 480), B("rs"), B("e1"))
         copy(B("d2", 16, 48), B("y1", 16, YW, 16))
         copy(B("lb"), B("c2", 15, 480, 16))
         for m in range(1, M):
             tti(B("d2", 16 + 32 * m, 48 + 32 * m), B("d2", 0, 16 + 32 * m), B("lb", 2 * m - 2, 2 * m), B("y1", 16 + m, YW, 16), OP.add)
             settled(m - 1)
-            for f in spare[:1]: f()
-            spare = spare[1:]
+            slot()
         settled(M - 1)
+        slot()
         scan(B("c2", 0, C), B("rs", 0, C), B("e2"))
+        slot()
         ts(B("dw"), B("c2", 15, C, 16), 1 / UNIT, OP.mult)
+        slot()
         ts(B("dm", 0, 24), B("dw"), 3, OP.bitwise_and)
-        ts(B("pos"), B("dm", 0, 24), 0.0, OP.is_gt)
-        tti(B("ind"), B("dm"), L("lcls"), B("cls"), OP.is_equal)
-        tt(B("ls"), B("sx", 72, 96), B("pos"), OP.mult)
+        slot()
+        for c in range(4): ts(B("ind", 32 * c, 32 * c + 32), B("dm"), float(c), OP.is_equal)
+        ts(B("ls"), B("dm", 0, 24), float(C), OP.mult)
         scan(B("inc"), B("rq"), B("ind"))
-        ts(B("ql%d" % t), B("ls"), float(C), OP.add)
-        send(2, t)
-        copyi(B("tb"), B("inc"), L("ltot"))
+        tt(B("pos"), B("ls"), B("ca", 48, 72), OP.add)
+        turn(B("tv"), B("inc"))
+        copy(B("lv"), B("pos"))
+        acti(B("jv"), B("jt"), B("lv"))
+        tt(B("w1", 1, 129), B("tv"), B("mk"), OP.mult)
         tt(B("pr"), B("ind"), B("inc"), OP.mult)
-        run("v", lambda: g.vector.transpose(ap(B("tv")), ap(B("tb"))), [B("tb")], [B("tv")])
+        scan(B("bs"), B("one", 0, 128), B("w1", 0, 128))
         tt(B("ps_"), B("pr", 0, 64), B("pr", 64, 128), OP.add)
-        tti(B("w1"), B("tv"), L("ldup"), B("mk"), OP.mult)
+        turn(B("tw"), B("bs"))
         tt(B("pu", 4, 120, 5), B("ps_", 0, 24), B("ps_", 32, 56), OP.add)
-        scan(B("bs"), B("w2"), B("w1"))
-        for c in range(4): ts(B("pu", c, 120, 5), B("ind", 32 * c, 32 * c + 24), B("bs", 64 * c + 31, 64 * c + 32), OP.mult)
+        copyi(B("base"), B("tw"), B("lsel", 0, 1))
+        slot()
+        for c in range(4): ts(B("pu", c, 120, 5), B("ind", 32 * c, 32 * c + 24), B("base", c, c + 1), OP.mult)
+        slot()
         scan(B("pv"), B("r5"), B("pu"))
+        slot()
         ts(B("lpl"), B("pv", 4, 120, 5), -1.0, OP.add)
         ts(B("lpx"), B("pv", 4, 120, 5), -1.0, OP.add, float(A), OP.min)
-        for k in range(4): expect(k, t)
-        for b in range(4):
-            mm(B("psA", 512 * b, 512 * b + C), side("nq", b), side("npl", b), B(aq), B(apl))
-            for name in ("fn", "fo")[:1 + (b < 2)]: act(body(name, b), B("psA", 512 * b, 512 * b + C))
-        for b in (2, 3): acti(body("mg", b), plane("fn", b), B(al))
-        for b in (0, 1): tti(B("pt", b, 4 * C, 4), plane("fn", b), B(al), body("fo", b), OP.subtract)
-        for b in (2, 3): tt(B("pt", b, 4 * C, 4), body("mg", b), B("psA", 512 * b, 512 * b + C), OP.subtract)
-        for h, ps in ((0, "psB"), (192, "psA")):
-            quant(B("pq", h, h + 192), B("pz", h, h + 192), B("pt", 4 * h, 4 * h + 768))
-            mm(B(ps, 0, 192), side("eq", 0), side("ep", 0), B("pq", h, h + 192), B("pz", h, h + 192))
-            act(B("ma", h, h + 192), B(ps, 0, 192))
-        for b in range(1, 4):
-            mm(B("psB", 512 * b, 512 * b + C), side("eq", b), side("ep", b), B("pq"), B("pz"))
-            act(body("ma", b), B("psB", 512 * b, 512 * b + C))
-            if b > 1: acti(body("mg", b), plane("ma", b), B(al))
-        run("v", lambda: g.vector.tensor_copy(ind(B("of"), B("lpl")), ap(B("jid"))), [B("jid"), B("lpl")], [B("of")])
-        order = [lambda: tt(B("og"), B("of", 0, A), B("dg", 0, A), OP.mult), lambda: scan(B("oh"), B("rs", 0, A), B("og")),
-                 lambda: ts(B("qo%d" % t), B("oh", 15, A, 16), 192.0, OP.add)]
-        for src, dst in (("ma", "mb"), ("mb", "mc"), ("mc", "mb")):
-            if src != "ma":
-                for b in (2, 3): acti(body("mg", b), plane(src, b), B(al))
-            for b in (0, 1):
-                if src == "ma":
-                    order[b]()
-                    copy(body("md", b), body("ma", b))
-                tti(body(dst, b), plane(src, b), B(al), body("md", b), OP.add)
-            if src == "ma":
-                order[2]()
-                send(3, t)
-            for b in (2, 3): tt(body(dst, b), body("mg", b), B("psB", 512 * b, 512 * b + C), OP.add)
-        for b in range(3): acti(B("mt", b, 4 * A, 4), plane("mb", b), B(ao))
-        acti(B("mt", 3, 640, 4), plane("mb", 3), B(ao, 0, 10))
-        copyi(B("mt", 643, 1280, 4), plane("mb", 3), B(ao, 10, 20))
+        run("v", lambda: g.vector.tensor_copy(ind(B("of"), B("lpl")), ap(B("jv"))), [B("jv"), B("lpl")], [B("of")])
+        tt(B("og"), B("of", 0, A), B("dg"), OP.mult)
+        slot()
+        scan(B("oh"), B("rs", 0, A), B("og"))
+        slot()
+        copy(B("qo%d" % t), B("oh", 15, A, 16))
+        send(3, t)
+        while jobs: slot()
+        mm(bank("psB", 3), side("eq", 3), side("ep", 3), B(tq), B(tp))
+        expect(3, t)
+        for b in range(4): (copyi if b % 2 else acti)(B("mt", b, 4 * A, 4), B("gm", 4 * C * b, 4 * C * b + 4 * C), B(ao))
         for h, ps in ((0, "psA"), (160, "psB")):
             quant(B("mq", h, h + 160), B("mp", h, h + 160), B("mt", 4 * h, 4 * h + 640))
             mm(B(ps, 0, 160), side("wq", 0), side("wp", 0), B("mq", h, h + 160), B("mp", h, h + 160))
             actm(B("rp", h, h + 160), B(ps, 0, 160), 0.015625)
         if t == R - 1: quant(B("vq"), B("vp"), B("vt"))
         for b in range(1, 4):
-            mm(B("psA", 512 * b, 512 * b + A), side("wq", b), side("wp", b), B("mq"), B("mp"))
-            actm(B("rp", RW * b, RW * b + A), B("psA", 512 * b, 512 * b + A), 0.015625)
-        for b in range(4):
-            tti(B("xt", b, 4 * C, 4), B("rp", RW * b, RW * b + RW), B("lpx"), body("fp", b), OP.add)
+            mm(bank("psA", b, A), side("wq", b), side("wp", b), B("mq"), B("mp"))
+            actm(B("rp", RW * b, RW * b + A), bank("psA", b, A), 0.015625)
+        acti(B("rg"), B("rp", RW * 3, RW * 3 + A + 1), B("lpx"))
+        for b in range(3): tti(B("xt", b, 4 * C, 4), B("rp", RW * b, RW * b + A + 1), B("lpx"), body("fp", b), OP.add)
+        tt(B("xt", 3, 4 * C, 4), B("rg"), bank("psB", 3), OP.add)
 
     quant(B("tq%d" % R), B("tp%d" % R), B("xt"))
-    pick(B("oq"), B("op"), B("tq%d" % R), B("tp%d" % R), B("lcb", 48, 72))
+    for h in (0, 192): pick(B("oq", h, h + 192), B("op", h, h + 192), B("tq%d" % R), B("tp%d" % R), B("lback", h // 16, h // 16 + 12))
+    for k, h in enumerate((0, 192)):
+        mm(bank("psA", k, 192), B("vq"), B("vp"), B("oq", h, h + 192), B("op", h, h + 192))
+        (copy if k else act)(B("yo", h, h + 192), bank("psA", k, 192))
     dma([("y", T.oc[:, :], T.oq[:, :].bitcast(dt.uint8))], [B("oq")], [])
+    dma([("s", T.y[:, 0:192], T.yo[:, 0:192])], [B("yo", 0, 192)], [])
     dma([("s", T.osc[4 * k:4 * k + 4, :], T.op[32 * k:32 * k + 4, :]) for k in range(4)], [B("op")], [])
-    mm(B("psB", 0, C), B("vq"), B("vp"), B("oq"), B("op"))
-    copy(B("yo"), B("psB", 0, C))
-    dma([("y", T.y[:, :], T.yo[:, :])], [B("yo")], [])
+    dma([("y", T.y[:, 192:C], T.yo[:, 192:C])], [B("yo", 192, C)], [])
     for s in sorted(count): g.wait_ge(T.sem[s], count[s])

@@ -5,10 +5,11 @@ STEP = [1, 2, 4]
 Q, M = 24, 16
 RW = 336
 YW = 528
-UNIT = 0.0009765625
+UNIT = 1024.0
 F4, U8 = "float8_e4m3fn_x4", "uint8"
 WHOLE = [(), (), ()]
-WAIT = [12, 0, 3, 0, 0]
+MORE = [1, 1, 1, 1]
+WAIT = [9, 1, 2, 0, 0]
 
 PATTERNS = [("lu", 16, [[16, 2], [32, 4], [0, 2]], 0), ("lnat", 24, [[1, 24]], 0), ("lrun", 8, [[24, 2], [1, 2], [0, 2]], 0),
             ("lpair", 4, [[32, 2], [8, 2]], 0), ("lown", 24, [[32, 12], [C, 2]], 0), ("first", 48, [[32, 12], [1000, 2], [0, 2]], -1000)]
@@ -19,22 +20,21 @@ for _s, _n, _p, _b in PATTERNS:
 LW = _a
 
 WIDTHS = {
-    "bfloat16": {"xt0": 4 * C, "ut": 512, "vt": 512, "one": 516, "et": 516, "ia": 480, "ib": A, "dg": A, "rs": 480, "rq": 128, "r5": 120,
-                 "hp": 128, "mk": 128, "fp": 4 * C, "fn": 4 * C, "ft": 4 * C,
-                 "pt": 4 * C, "gm": 16 * C, "mg": 8 * C, "md": 4 * C, "mt": 4 * A, "xt": 4 * C},
-    "float32": {"jt": 4 * C, "jv": C, "of": C, "og": A, "oh": A, "zero": 16, "tbl": 800, "i6": C, "sb": 2 * C, "c1": 1152, "c2": 1152, "e1": 480, "e2": C, "cb": 72, "b1": 128, "b2": 128,
-                "y1": YW, "d2": YW, "ind": 128, "inc": 128, "tv": 128, "w1": 132, "bs": 128, "tw": 128, "pu": 120, "pv": 120, "rp": 4 * RW,
-                "rg": C, "yo": C},
+    "bfloat16": {"xt0": 4 * C, "ut": 512, "vt": 512, "one": 516, "et": 516, "ia": C, "ib": 16, "dg": 16, "rs": C, "rq": 128, "r9": 216, "r10": 150,
+                 "fp": 4 * C, "ft": 4 * C, "pt": 4 * C, "gm": 16 * C, "mg": 8 * C, "md": 4 * C, "mt": 4 * A, "xt": 4 * C},
+    "float32": {"jt": 4 * C, "jv": C, "of": 16 + C, "og": 2 * A + 32, "zero": 16, "tbl": 800, "i6": C, "sb": 2 * C, "c1": 1152, "c2": 1152, "e1": 410,
+                "e2": C, "cb": 72, "b1": 128, "b2": 128, "y1": YW, "d2": YW, "ind": 128, "inc": 128, "tv": 136, "bs": 128, "tw": 128, "pu": 216, "pv": 216,
+                "rp": 4 * RW, "rg": C, "yo": C},
     "int32": {"ca": 72, "dw": 24, "dm": 32, "pi": 1, "pm": 3, "li": LW, "k1": 72, "k2": 72, "k3": 72, "ke": 48},
-    "uint16": {"lu": 16, "lnat": 24, "lrun": 8, "lpair": 8, "lsel": 2, "lback": 24, "lc": 72, "lie": 48, "lb": 30, "lpl": 24, "lpx": 24, "lv": 24},
+    "uint16": {"lu": 16, "lnat": 24, "lrun": 8, "lpair": 8, "lsel": 2, "lback": 24, "lc": 72, "lie": 50, "lb": 30, "lpl": 24, "lpx": 24, "lv": 24},
     F4: {"wq": 512, "uq": 128, "urq": 256, "vq": 128, "xq": C, "eq": 512, "fq": C, "pq": C, "mq": A, "oq": C},
     U8: {"wp": 512, "up": 128, "urp": 256, "vp": 128, "xp": C, "ep": 512, "fz": C, "pz": C, "mp": A, "op": C},
 }
 SCRATCH = {n: ("sbuf", [128, w], k) for k, m in WIDTHS.items() for n, w in m.items()}
 PART, _a = {}, 0
-for _s, _n in {"fc": 3, "mh": 1, "t1": 1, "z1": 1, "t2": 1, "t3": 1, "t4": 1, "m24": 1, "up384": 1, "even": 1, "fr": 1, "fs": 48, "kb": 112, "kc": 112,
-               "kd": 112, "da": 48, "db": 48, "dc": 48, "se": 24, "sm": 96, "sx": 96, "gg": 24, "sel": 192, "seld": 96, "kf": 48, "kg": 48,
-               "ks": 48, "kt": 48, "ls": 24, "pos": 24, "ps_": 64, "pr": 128, "base": 16}.items():
+for _s, _n in {"fc": 3, "mh": 1, "t1": 1, "z1": 1, "t2": 1, "t3": 1, "t4": 2, "m24": 1, "up384": 1, "even": 1, "fr": 1, "high": 1, "low": 1, "sign": 1,
+               "fs": 48, "kb": 112, "kc": 112, "kd": 112, "da": 48, "db": 48, "dc": 48, "sk": 192, "sx": 192, "sy": 48, "sel": 192, "kf": 48, "kg": 48,
+               "ks": 48, "kt": 48, "ls": 24, "pos": 24, "ps_": 64, "pr": 128, "dl": 32}.items():
     PART[_s] = (_a, _a + _n)
     _a += _n
 SCRATCH["small"] = ("sbuf", [128, _a], "float32")
@@ -42,10 +42,10 @@ SCRATCH["psA"] = SCRATCH["psB"] = ("psum", [128, 2048], "float32")
 for _t in range(R + 1):
     SCRATCH["tq%d" % _t] = ("sbuf", [128, C], F4)
     SCRATCH["tp%d" % _t] = ("sbuf", [128, C], U8)
-SENT = [("tq", "aq", F4, C), ("tp", "ap", U8, C), ("ql", "al", "uint16", 24), ("qo", "ao", "uint16", 20)]
+SENT = [("tq", "aq", F4, C), ("tp", "ap", U8, C), ("ql", "al", "uint16", 5 * Q), ("qo", "ao", "uint16", 20)]
 for _t in range(R):
     for _s, _d, _k, _n in SENT:
-        if _s[0] == "q": SCRATCH["%s%d" % (_s, _t)] = ("sbuf", [128, _n], _k)
+        if _s[0] == "q": SCRATCH["%s%d" % (_s, _t)] = ("sbuf", [128, max(_n, 32)], _k)
         SCRATCH["%s%d" % (_d, _t)] = ("sbuf", [128, _n], _k)
 NDMA = 12
 SEMAPHORES = ["cv", "cs", "ct", "cg"] + ["d%d" % k for k in range(NDMA)] + ["%s_%s%d" % (a, b[0][1], t) for a in ("r", "l") for b in SENT for t in range(R)]
@@ -129,6 +129,7 @@ def rank_program(g, core, T, topo):
     def ts(out, a, s1, op, s2=None, op1=None):
         if op1 is None: run("v", lambda: g.vector.tensor_scalar(ap(out), ap(a), sc(s1), None, op), [a] + rd(s1), [out])
         else: run("v", lambda: g.vector.tensor_scalar(ap(out), ap(a), sc(s1), sc(s2), op, op1), [a] + rd(s1, s2), [out])
+    def tsi(out, a, off, s): run("v", lambda: g.vector.tensor_scalar(ap(out), ind(a, off), ap(s), None, OP.mult), [a, off, s], [out])
     def scan(out, keep, a): run("v", lambda: g.vector.tensor_tensor_scan(ap(out), ap(keep), ap(a), 0.0, OP.mult, OP.add), [keep, a], [out])
     def turn(out, i): run("v", lambda: g.vector.transpose(ap(out), ap(i)), [i], [out])
     def quant(q, p, i): run("v", lambda: g.vector.quantize_mx(ap(q), ap(p), ap(i)), [i], [q, p])
@@ -157,7 +158,7 @@ def rank_program(g, core, T, topo):
         s, d, kind, n = SENT[k]
         dst, src = T.cores[(rank + STEP[t]) % N], "%s%d" % (s, t)
         settle("g", [B(src)], [])
-        i, o = T[src][:, :], T["%s%d" % (d, t)][:, :]
+        i, o = T[src][:, 0:n], T["%s%d" % (d, t)][:, :]
         if kind == F4: i, o = i.bitcast(dt.uint8), o.bitcast(dt.uint8)
         ls, to = "l_%s%d" % (s[1], t), topo.addr(dst)
         g.remote_dma(o, i, T.sem["r_%s%d" % (s[1], t)], T.sem[ls], to[1], to[0], topo.mask(core, dst))
@@ -196,16 +197,16 @@ def rank_program(g, core, T, topo):
     ts(B("m24"), pm, float(Q), OP.mult)
     ts(B("t1"), odd, 16.0, OP.mult, mh, OP.add)
     ts(B("lrun"), L("lrun"), mh, OP.add, pm, OP.add)
-    ts(B("t2"), odd, 64.0, OP.mult, mh, OP.add)
+    ts(B("even"), odd, -1.0, OP.mult, 1.0, OP.add)
     ts(B("z1"), po, 4.0, OP.mult, B("t1"), OP.add)
     ts(B("lnat"), L("lnat"), B("m24"), OP.add)
-    ts(B("lpair", 4, 8), L("lpair"), B("t2"), OP.add, po, OP.add)
+    ts(B("t2"), B("even"), 64.0, OP.mult, mh, OP.add)
     ts(B("lpair", 0, 4), L("lpair"), B("z1"), OP.add)
-    ts(B("even"), odd, -1.0, OP.mult, 1.0, OP.add)
+    ts(B("lpair", 4, 8), L("lpair"), B("t2"), OP.add, po, OP.add)
     ts(B("lc", 48, 72), L("lown"), pm, OP.add, po, OP.add)
     keep(B("et"), B("one"), [[1, 516]], OP.is_equal, -3, -4)
     iotaf(B("i6"), [[1, 24], [32, 16]], 16, 0)
-    iotaf(B("ia"), [[0, 30], [1, 16]], 0, 0)
+    iotaf(B("ia"), [[0, 24], [1, 16]], 0, 0)
 
     ts(B("k1"), B("ca"), 1 / Q, OP.mult, -0.479, OP.add)
     ts(B("k3"), B("ca"), 16.0, OP.mult, up, OP.add)
@@ -221,9 +222,9 @@ def rank_program(g, core, T, topo):
     for b in (2, 3): quant(side("eq", b), side("ep", b), B("et", 3 - b, 515 - b))
     copyi(B("b1"), B("b2"), B("lpair"))
     act(B("tbl", C, 400), B("zero"))
-    actf(B("tbl", 386, 387), B("zero", 0, 1), AF.Identity, 1.0, UNIT)
-    actf(B("tbl", 0, C), B("i6"), AF.Identity, 1.0, UNIT)
-    actf(B("tbl", 400, 800), B("tbl", 0, 400), AF.Identity, 1.0, UNIT)
+    actf(B("tbl", 386, 387), B("zero", 0, 1), AF.Identity, 1.0, 1.0)
+    actf(B("tbl", 0, C), B("i6"), AF.Identity, UNIT, 1.0)
+    actf(B("tbl", 400, 800), B("tbl", 0, 400), AF.Identity, 1.0, 1.0)
     act(B("y1", 0, 16), B("zero"))
     quant(B("xq"), B("xp"), B("xt0"))
     pick(B("tq0"), B("tp0"), B("xq"), B("xp"), B("lnat"))
@@ -238,34 +239,35 @@ def rank_program(g, core, T, topo):
 
     def lists_inside():
         k2, k3 = B("k2", 0, 48), B("k3", 0, 48)
-        ts(k2, B("ke"), 15, OP.bitwise_and)
-        tt(B("sel", 96, 144), B("ke"), B("fs"), OP.is_equal)
-        ts(k3, B("ke"), 16.0, OP.add)
-        ts(B("kf"), k2, pm, OP.is_equal, 386.0, OP.mult)
-        ts(B("ks"), B("sel", 96, 144), 400.0, OP.mult)
-        tt(B("kt"), B("kf"), B("ke"), OP.max)
-        ts(B("sel", 144, 192), B("ke"), C - 1.0, OP.min)
-        tt(B("sel", 48, 96), B("kt"), B("ks"), OP.max)
-        ts(B("kg"), B("sel", 48, 96), 386.0, OP.is_equal, 1000.0, OP.mult)
-        tt(B("sel", 0, 48), B("kg"), k3, OP.min)
-        tt(B("seld"), B("sel", 1, 192, 2), B("sel", 0, 192, 2), OP.subtract)
+        levels = [[lambda: ts(k2, B("ke"), 15, OP.bitwise_and), lambda: tt(B("sel", 96, 144), B("ke"), B("fs"), OP.is_equal)],
+                  [lambda: ts(B("kf"), k2, pm, OP.is_equal, 386.0, OP.mult), lambda: ts(B("ks"), B("sel", 96, 144), 400.0, OP.mult)],
+                  [lambda: tt(B("kt"), B("kf"), B("ke"), OP.max), lambda: ts(B("sel", 144, 192), B("ke"), C - 1.0, OP.min)],
+                  [lambda: tt(B("sel", 48, 96), B("kt"), B("ks"), OP.max), lambda: ts(k3, B("ke"), 16.0, OP.add)],
+                  [lambda: ts(B("kg"), B("sel", 48, 96), 386.0, OP.is_equal, 1000.0, OP.mult)],
+                  [lambda: tt(B("sel", 0, 48), B("kg"), k3, OP.min)],
+                  [lambda: tt(B("sel", 0, 192, 2), B("sel", 0, 192, 2), B("sel", 1, 192, 2), OP.subtract)]]
+        jobs.extend([lambda fs=fs: [f() for f in fs] for fs in levels])
 
     def late_constants():
-        actf(B("ib"), B("ia", 0, A), AF.Abs, -1.0, pm)
-        actf(B("dg"), B("ib"), AF.Relu, -1.0, 1.0)
-        iotaf(B("hp"), [[0, 4], [1, 2], [0, 16]], 0, 0)
-        keep(B("rq"), B("one", 0, 128), [[0, 4], [1, 32]], OP.not_equal, 0, 0)
-        keep(B("r5"), B("one", 0, 120), [[0, 24], [1, 5]], OP.not_equal, 0, 0)
-        actm(B("e1"), B("one", 0, 480), 0.0)
+        actm(B("sk", 0, 192, 2), B("one", 0, 96), 0.0)
+        actf(B("ib"), B("ia", 0, 16), AF.Abs, -1.0, pm)
         actm(B("y1", 400, YW), B("one", 0, YW - 400), 0.0)
-        act(B("d2", 0, 16), B("zero"))
+        actf(B("dg"), B("ib"), AF.Relu, -1.0, 1.0)
+        keep(B("r10"), B("one", 0, 150), [[0, 15], [1, 10]], OP.not_equal, 0, 0)
+        keep(B("rq"), B("one", 0, 128), [[0, 4], [1, 32]], OP.not_equal, 0, 0)
+        keep(B("r9"), B("one", 0, 216), [[0, 24], [1, 9]], OP.not_equal, 0, 0)
         actf(B("rs"), B("ia"), AF.Sign, 1.0, 0.0)
+        actm(B("high"), po, 1 / 16)
+        for name in ("d2", "of"): act(B(name, 0, 16), B("zero"))
         act(B("rp", A, 4 * RW, RW), B("zero", 0, 4))
-        act(B("w1", 0, 1), B("zero", 0, 1))
-        actf(B("mk"), B("hp"), AF.Abs, -1.0, odd)
+        act(B("tv", 7, 8), B("zero", 0, 1))
+        actf(B("sign"), B("high"), AF.Identity, -2.0, 1.0)
+        actf(B("low"), B("high"), AF.Identity, -1.0, 1.0)
+        actf(B("rq", 31, 128, 32), B("zero", 0, 4), AF.Identity, 1.0, B("low"))
 
     def leave(k):
-        for q in (k // 16, k // 16 + 1): ts(B("e1", q, 480, 32), B("y1", 17 + 16 * q, 32 + 16 * q), B("dg", q % 16, q % 16 + 1), OP.mult)
+        for q in (k // 16, k // 16 + 1):
+            ts(B("e1", q, 240, 16) if q < 16 else B("e1", 234 + q, 400, 10), B("y1", 17 + 16 * q, 32 + 16 * q), B("dg", q % 16, q % 16 + 1), OP.mult)
 
     def settled(m):
         ts(B("e2", m, C, 16), B("d2", 16 + 32 * m, 40 + 32 * m), B("dg", m, m + 1), OP.mult)
@@ -288,19 +290,17 @@ def rank_program(g, core, T, topo):
         def columns():
             for x in range(2): expect(x, t)
             unpack("psA", aq, apl)
-            for b in range(4):
-                act(body("fn", b), bank("psA", b))
-                act(B("ft", b, 4 * C, 4), bank("psA", b))
+            for b in range(4): act(B("ft", b, 4 * C, 4), bank("psA", b))
 
         def roots(h):
             quant(B("fq", h, h + 192), B("fz", h, h + 192), B("ft", 4 * h, 4 * h + 768))
             if h:
                 unpack("psB", "fq", "fz")
                 expect(2, t)
-                for b in range(4): acti(near(b, 0), body("fn", b), B(al))
+                for b in range(4): acti(near(b, 0), B("ft"), B(al, Q * b + Q, Q * b + 2 * Q))
                 for b in range(4): act(made(b, 0), bank("psB", b))
                 for b in range(4):
-                    if b not in WHOLE[0]: acti(near(b, 1), made(b, 0), B(al))
+                    if b not in WHOLE[0]: acti(near(b, 1), made(b, 0), B(al, 0, Q))
 
         def pack(h):
             quant(B("pq", h, h + 192), B("pz", h, h + 192), B("pt", 4 * h, 4 * h + 768))
@@ -311,12 +311,12 @@ def rank_program(g, core, T, topo):
         def step(d, b, h):
             if b in WHOLE[d - 1]: tti(made(b, d, h, h + 192), made(b, d - 1), B(al, h // 16, h // 16 + 12), B("md", C * b + h, C * b + h + 192), OP.add)
             else: tt(made(b, d, h, h + 192), near(b, d, h, h + 192), half("psB", b, h), OP.add)
-            if h and d < 3 and b not in WHOLE[d]: acti(near(b, d + 1), made(b, d), B(al))
+            if h and d < 3 and b not in WHOLE[d]: acti(near(b, d + 1), made(b, d), B(al, 0, Q))
 
         columns()
         if t == 0:
-            jobs.extend([lambda: fill(B("dm"), 9.0), lambda: ts(B("t3"), pm, 3.0, OP.min, 32.0, OP.mult),
-                         lambda: ts(B("t4"), po, -1 / 16, OP.mult, 31.0, OP.add), lambda: ts(B("lsel", 0, 1), B("t3"), B("t4"), OP.add),
+            jobs.extend([lambda: fill(B("dm"), 9.0), lambda: ts(B("t3"), odd, B("high"), OP.not_equal, A + 16.0, OP.mult),
+                         lambda: ts(B("t4"), B("ca", 48, 50), 16.0, OP.mult, B("t3"), OP.add), lambda: ts(B("lsel"), B("t4"), 2.0 * A, OP.min),
                          lambda: ts(B("lback"), B("cb", 48, 72), up, OP.subtract)])
         wait(WAIT[0] - len(jobs))
         jobs.extend([lambda h=h: roots(h) for h in (0, 192)])
@@ -342,46 +342,60 @@ def rank_program(g, core, T, topo):
         copy(B("sb", C + 192, 2 * C), bank("psA", 3, 192))
         if t == 0: lists_inside()
         for k in (1, 2): acti(B("c1", C * k, C * k + C), B("sb"), B("lc", Q * k, Q * k + Q))
+        slot()
         copyi(B("c1", 0, C), B("sb"), B("lc", 0, Q))
         if t == 0: late_constants()
         unpack("psB", tq, tp)
         for b in range(4): act(body("fp", b), bank("psB", b))
-        for k in range(3): turn(B("c2", C * k, C * k + C), B("c1", C * k, C * k + C))
+        for k in range(3):
+            slot()
+            turn(B("c2", C * k, C * k + C), B("c1", C * k, C * k + C))
+        slot()
         for h in (0, 1): tt(B("da", 24 * h, 24 * h + 24), B("c2", 16 * h, 768, 32), B("c2", 768, 1152, 16), OP.subtract)
         for h in (0, 1): tt(B("db", 24 * h, 24 * h + 24), B("c2", 768, 1152, 16), B("c2", 16 * h, 768, 32), OP.subtract)
+        slot()
         tt(B("dc"), B("da"), B("db"), OP.max)
-        tt(B("se"), B("dc", 24, 48), B("dc", 0, 24), OP.is_lt)
-        for h in (0, 24, 48): tt(B("sm", h, h + 24), B("seld", h, h + 24), B("se"), OP.mult)
-        tt(B("sx", 0, 72), B("sm", 0, 72), B("sel", 0, 144, 2), OP.add)
-        tt(B("sm", 72, 96), B("seld", 72, 96), B("se"), OP.mult)
-        for h in (0, 12): tt(B("gg", h, h + 12), B("sx", 49, 72, 2), B("sx", 2 * h, 2 * h + 24, 2), OP.mult)
-        tt(B("sx", 72, 96), B("sm", 72, 96), B("sel", 144, 192, 2), OP.add)
-        tt(B("sx", 1, 48, 2), B("sx", 1, 48, 2), B("gg"), OP.add)
-        copy(B("ql%d" % t), B("sx", 72, 96))
+        slot()
+        for h in range(0, 192, 48): tt(B("sk", h + 1, h + 48, 2), B("dc", 24, 48), B("dc", 0, 24), OP.is_lt)
+        scan(B("sx", 0, 144), B("sk", 0, 144), B("sel", 0, 144))
+        scan(B("sx", 144, 192), B("sk", 144, 192), B("sel", 144, 192))
+        for h in (1, 0): scan(B("sy", 24 * h, 24 * h + 24), B("sx", 97, 144, 2), B("sx", 48 * h + 1, 48 * h + 48, 2))
+        copy(B("ql%d" % t, 0, Q), B("sx", 145, 192, 2))
+        for b in (0, 1): ts(B("ql%d" % t, Q * b + Q, Q * b + 2 * Q), B("sx", 145, 192, 2), 4.0, OP.mult, float(b), OP.add)
+        copy(B("lie", 0, 48), B("sy"))
+        for b in (2, 3): ts(B("ql%d" % t, Q * b + Q, Q * b + 2 * Q), B("sx", 145, 192, 2), 4.0, OP.mult, float(b), OP.add)
         send(2, t)
-        copy(B("lie"), B("sx", 0, 48))
+        copy(B("lie", 48, 49), B("sy", 23, 24))
         copyi(B("y1", 16, 80), B("tbl"), B("lie", 24, 28))
         for x, y in ((4, 10), (10, 24)): acti(B("y1", 16 + 16 * x, 16 + 16 * y), B("tbl"), B("lie", 24 + x, 24 + y))
         if t == 0: iotaf(B("jt"), [[1, 4 * C]], 0, 0)
         rebuild(t)
         for k in range(32, C, 32):
-            tti(B("y1", 16 + k, 48 + k), B("y1", 0, 16 + k), B("lie", k // 16, k // 16 + 2), B("y1", 16 + k, 48 + k), OP.add)
+            if k == C - 32:
+                for s in (0, 1): tsi(B("e1", 248 + s, 408, 10), B("y1", 0, 16 + k), B("lie", 22 + 26 * s, 23 + 26 * s), B("dg", 6 + s, 7 + s))
+            else:
+                tti(B("y1", 16 + k, 48 + k), B("y1", 0, 16 + k), B("lie", k // 16, k // 16 + 2), B("y1", 16 + k, 48 + k), OP.add)
             leave(k - 32)
-            slot()
-        leave(C - 32)
+            if k == 224: leave(C - 32)
+            if k == 288: scan(B("c2", 0, 240), B("rs", 0, 240), B("e1", 0, 240))
+            elif k == 320: ts(B("lb", 0, 30, 2), B("c2", 15, 240, 16), 1 / UNIT, OP.mult)
+            else: slot()
+        tti(B("y1", 16 + k, 48 + k), B("y1", 0, 16 + k), B("lie", k // 16, k // 16 + 2), B("y1", 16 + k, 48 + k), OP.add)
+        scan(B("c2", 240, 390), B("r10"), B("e1", 250, 400))
         slot()
-        scan(B("c2", 0, 480), B("rs"), B("e1"))
         copy(B("d2", 16, 48), B("y1", 16, YW, 16))
-        copy(B("lb"), B("c2", 15, 480, 16))
-        for m in range(1, M):
+        ts(B("lb", 1, 30, 2), B("c2", 249, 390, 10), 1 / UNIT, OP.mult)
+        ts(B("e2", M - 1, C, 16), B("y1", 15 + M, 400, 16), B("dg", M - 1, M), OP.mult)
+        for m in range(1, M - 1):
             tti(B("d2", 16 + 32 * m, 48 + 32 * m), B("d2", 0, 16 + 32 * m), B("lb", 2 * m - 2, 2 * m), B("y1", 16 + m, YW, 16), OP.add)
             settled(m - 1)
             slot()
-        settled(M - 1)
+        settled(M - 2)
+        tsi(B("dl"), B("d2", 0, 496), B("lb", 28, 30), B("dg", M - 1, M))
         slot()
         scan(B("c2", 0, C), B("rs", 0, C), B("e2"))
         slot()
-        ts(B("dw"), B("c2", 15, C, 16), 1 / UNIT, OP.mult)
+        tt(B("dw"), B("c2", 15, C, 16), B("dl", 0, 24), OP.add)
         slot()
         ts(B("dm", 0, 24), B("dw"), 3, OP.bitwise_and)
         slot()
@@ -389,29 +403,32 @@ def rank_program(g, core, T, topo):
         ts(B("ls"), B("dm", 0, 24), float(C), OP.mult)
         scan(B("inc"), B("rq"), B("ind"))
         tt(B("pos"), B("ls"), B("ca", 48, 72), OP.add)
-        turn(B("tv"), B("inc"))
+        if MORE[0]: slot()
+        turn(B("tv", 8, 136), B("inc"))
         copy(B("lv"), B("pos"))
         acti(B("jv"), B("jt"), B("lv"))
-        tt(B("w1", 1, 129), B("tv"), B("mk"), OP.mult)
         tt(B("pr"), B("ind"), B("inc"), OP.mult)
-        scan(B("bs"), B("one", 0, 128), B("w1", 0, 128))
+        scan(B("bs"), B("one", 0, 128), B("tv", 7, 135))
         tt(B("ps_"), B("pr", 0, 64), B("pr", 64, 128), OP.add)
+        if MORE[1]: slot()
         turn(B("tw"), B("bs"))
-        tt(B("pu", 4, 120, 5), B("ps_", 0, 24), B("ps_", 32, 56), OP.add)
-        copyi(B("base"), B("tw"), B("lsel", 0, 1))
+        tt(B("pu", 8, 216, 9), B("ps_", 0, 24), B("ps_", 32, 56), OP.add)
+        if MORE[2]: slot()
+        for c in range(8):
+            x = 32 * (c // 2)
+            ts(B("pu", c, 216, 9), B("ind", x, x + 24), B("tw", x + 30 + c % 2, x + 31 + c % 2), OP.mult, B("sign" if c % 2 else "high"), OP.mult)
         slot()
-        for c in range(4): ts(B("pu", c, 120, 5), B("ind", 32 * c, 32 * c + 24), B("base", c, c + 1), OP.mult)
+        scan(B("pv"), B("r9"), B("pu"))
         slot()
-        scan(B("pv"), B("r5"), B("pu"))
+        ts(B("lpl"), B("pv", 8, 216, 9), -1.0, OP.add)
+        ts(B("lpx"), B("pv", 8, 216, 9), -1.0, OP.add, float(A), OP.min)
+        if MORE[3]: slot()
+        run("v", lambda: g.vector.tensor_copy(ind(B("of", 16), B("lpl")), ap(B("jv"))), [B("jv"), B("lpl")], [B("of", 16)])
         slot()
-        ts(B("lpl"), B("pv", 4, 120, 5), -1.0, OP.add)
-        ts(B("lpx"), B("pv", 4, 120, 5), -1.0, OP.add, float(A), OP.min)
-        run("v", lambda: g.vector.tensor_copy(ind(B("of"), B("lpl")), ap(B("jv"))), [B("jv"), B("lpl")], [B("of")])
-        tt(B("og"), B("of", 0, A), B("dg"), OP.mult)
+        turn(B("og", 0, A), B("of", 16, 16 + A))
+        turn(B("og", A), B("of", 0, A + 32))
         slot()
-        scan(B("oh"), B("rs", 0, A), B("og"))
-        slot()
-        copy(B("qo%d" % t), B("oh", 15, A, 16))
+        copyi(B("qo%d" % t), B("og"), B("lsel"))
         send(3, t)
         while jobs: slot()
         mm(bank("psB", 3), side("eq", 3), side("ep", 3), B(tq), B(tp))

from concourse.mybir import dt, AluOpType, ActivationFunctionType

C, A, R, N = 384, 320, 3, 8
STEP = [1, 2, 4]
Q, M = 24, 16
RW = 336
YW = 528
UNIT = 1024.0
F4, U8 = "float8_e4m3fn_x4", "uint8"
WHOLE = [(), (), ()]
MORE = [1, 1, 1, 1]
WAIT = [9, 1, 2, 0, 0]

PATTERNS = [("lu", 16, [[16, 2], [32, 4], [0, 2]], 0), ("lnat", 24, [[1, 24]], 0), ("lrun", 8, [[24, 2], [1, 2], [0, 2]], 0),
            ("lpair", 4, [[32, 2], [8, 2]], 0), ("lown", 24, [[32, 12], [C, 2]], 0), ("first", 48, [[32, 12], [1000, 2], [0, 2]], -1000)]
LAT, _a = {}, 0
for _s, _n, _p, _b in PATTERNS:
    LAT[_s] = (_a, _a + _n)
    _a += _n
LW = _a

WIDTHS = {
    "bfloat16": {"xt0": 4 * C, "ut": 512, "vt": 512, "one": 516, "et": 516, "ia": C, "ib": 16, "dg": 16, "rs": C, "rq": 128, "r9": 216, "r10": 150,
                 "fp": 4 * C, "ft": 4 * C, "pt": 4 * C, "gm": 16 * C, "mg": 8 * C, "md": 4 * C, "mt": 4 * A, "xt": 4 * C},
    "float32": {"jt": 4 * C, "jv": C, "of": 16 + C, "og": 2 * A + 32, "zero": 16, "tbl": 800, "i6": C, "sb": 2 * C, "c1": 1152, "c2": 1152, "e1": 410,
                "e2": C, "cb": 72, "b1": 128, "b2": 128, "y1": YW, "d2": YW, "ind": 128, "inc": 128, "tv": 136, "bs": 128, "tw": 128, "pu": 216, "pv": 216,
                "rp": 4 * RW, "rg": C, "yo": C},
    "int32": {"ca": 72, "dw": 24, "dm": 32, "pi": 1, "pm": 3, "li": LW, "k1": 72, "k2": 72, "k3": 72, "ke": 48},
    "uint16": {"lu": 16, "lnat": 24, "lrun": 8, "lpair": 8, "lsel": 2, "lback": 24, "lc": 72, "lie": 50, "lb": 30, "lpl": 24, "lpx": 24, "lv": 24},
    F4: {"wq": 512, "uq": 128, "urq": 256, "vq": 128, "xq": C, "eq": 512, "fq": C, "pq": C, "mq": A, "oq": C},
    U8: {"wp": 512, "up": 128, "urp": 256, "vp": 128, "xp": C, "ep": 512, "fz": C, "pz": C, "mp": A, "op": C},
}
SCRATCH = {n: ("sbuf", [128, w], k) for k, m in WIDTHS.items() for n, w in m.items()}
PART, _a = {}, 0
for _s, _n in {"fc": 3, "mh": 1, "t1": 1, "z1": 1, "t2": 1, "t3": 1, "t4": 2, "m24": 1, "up384": 1, "even": 1, "fr": 1, "high": 1, "low": 1, "sign": 1,
               "fs": 48, "kb": 112, "kc": 112, "kd": 112, "da": 48, "db": 48, "dc": 48, "sk": 192, "sx": 192, "sy": 48, "sel": 192, "kf": 48, "kg": 48,
               "ks": 48, "kt": 48, "ls": 24, "pos": 24, "ps_": 64, "pr": 128, "dl": 32}.items():
    PART[_s] = (_a, _a + _n)
    _a += _n
SCRATCH["small"] = ("sbuf", [128, _a], "float32")
SCRATCH["psA"] = SCRATCH["psB"] = ("psum", [128, 2048], "float32")
for _t in range(R + 1):
    SCRATCH["tq%d" % _t] = ("sbuf", [128, C], F4)
    SCRATCH["tp%d" % _t] = ("sbuf", [128, C], U8)
SENT = [("tq", "aq", F4, C), ("tp", "ap", U8, C), ("ql", "al", "uint16", 5 * Q), ("qo", "ao", "uint16", 20)]
for _t in range(R):
    for _s, _d, _k, _n in SENT:
        if _s[0] == "q": SCRATCH["%s%d" % (_s, _t)] = ("sbuf", [128, max(_n, 32)], _k)
        SCRATCH["%s%d" % (_d, _t)] = ("sbuf", [128, _n], _k)
NDMA = 12
SEMAPHORES = ["cv", "cs", "ct", "cg"] + ["d%d" % k for k in range(NDMA)] + ["%s_%s%d" % (a, b[0][1], t) for a in ("r", "l") for b in SENT for t in range(R)]


def rank_program(g, core, T, topo):
    rank = T.rank_of(core)
    if rank is None:
        return
    OP, AF = AluOpType, ActivationFunctionType
    eng = {"v": g.vector, "s": g.scalar, "t": g.tensor, "g": g, "y": g.sync}
    csem = {"v": "cv", "s": "cs", "t": "ct", "g": "cg"}
    count = {}
    known = {q: {} for q in eng}
    known["far"] = {}
    log = {}
    serial = [0]

    def apart(r, o):
        if r[2] <= o[1] or o[2] <= r[1]: return True
        if r[3] > 1 and r[3] == o[3]: return (r[1] - o[1]) % r[3] != 0
        for s, n in ((r, o), (o, r)):
            if n[3] == 1 and s[3] > 1 and (s[1] - n[1]) % s[3] >= n[2] - n[1]: return True
        return False

    def psum(r): return r[0] in ("psA", "psB")

    def widen(r):
        return (r[0], r[1] // 512 * 512, (r[2] + 511) // 512 * 512, 1) if psum(r) else r

    def settle(q, reads, writes):
        need = {}
        for w, rs in ((False, reads), (True, writes)):
            for r in rs:
                for o in log.get(r[0], ()):
                    if apart(widen(r), o["r"]): continue
                    if not (w or o["w"]) and not (psum(r) and o["q"] != q): continue
                    need[o["n"]] = o
        for n in sorted(need, reverse=True):
            o = need[n]
            if known[q].get(o["sem"], 0) >= o["val"]: continue
            eng[q].wait_ge(T.sem[o["sem"]], o["val"])
            for k, v in list(o["clock"].items()) + [(o["sem"], o["val"])]:
                known[q][k] = max(known[q].get(k, 0), v)

    def note(q, reads, writes, sem, val):
        serial[0] += 1
        clock = dict(known[q])
        for w, rs in ((False, reads), (True, writes)):
            for r in rs:
                r = widen(r)
                old = log.get(r[0], [])
                if w and r[3] == 1: old = [o for o in old if not (r[1] <= o["r"][1] and o["r"][2] <= r[2])]
                log[r[0]] = old + [{"r": r, "w": w, "q": q, "sem": sem, "val": val, "clock": clock, "n": serial[0]}]

    def run(q, call, reads, writes):
        settle(q, reads, writes)
        s = csem[q]
        count[s] = count.get(s, 0) + 1
        call().then_inc(T.sem[s], 1)
        note(q, reads, writes, s, count[s])

    def B(name, a=0, b=None, step=1):
        x, y = PART.get(name, (0, 0))
        return ("small", x + a, y if b is None else x + b, step) if y else (name, a, SCRATCH[name][1][1] if b is None else b, step)

    def L(name): return B("li", LAT[name][0], LAT[name][1])

    def ap(r):
        return T[r[0]][:, r[1]:r[2]] if r[3] == 1 else T[r[0]][:, r[1]:r[2]:r[3]]

    def ind(r, off): return ap(r).indirect(ap(off))
    def sc(x): return ap(x) if isinstance(x, tuple) else x
    def rd(*xs): return [x for x in xs if isinstance(x, tuple)]

    def fill(out, c): run("v", lambda: g.vector.memset(ap(out), c), [], [out])
    def copy(out, i): run("v", lambda: g.vector.tensor_copy(ap(out), ap(i)), [i], [out])
    def copyi(out, i, off): run("v", lambda: g.vector.tensor_copy(ap(out), ind(i, off)), [i, off], [out])
    def tt(out, a, b, op): run("v", lambda: g.vector.tensor_tensor(ap(out), ap(a), ap(b), op), [a, b], [out])
    def tti(out, a, off, b, op): run("v", lambda: g.vector.tensor_tensor(ap(out), ind(a, off), ap(b), op), [a, off, b], [out])
    def ts(out, a, s1, op, s2=None, op1=None):
        if op1 is None: run("v", lambda: g.vector.tensor_scalar(ap(out), ap(a), sc(s1), None, op), [a] + rd(s1), [out])
        else: run("v", lambda: g.vector.tensor_scalar(ap(out), ap(a), sc(s1), sc(s2), op, op1), [a] + rd(s1, s2), [out])
    def tsi(out, a, off, s): run("v", lambda: g.vector.tensor_scalar(ap(out), ind(a, off), ap(s), None, OP.mult), [a, off, s], [out])
    def scan(out, keep, a): run("v", lambda: g.vector.tensor_tensor_scan(ap(out), ap(keep), ap(a), 0.0, OP.mult, OP.add), [keep, a], [out])
    def turn(out, i): run("v", lambda: g.vector.transpose(ap(out), ap(i)), [i], [out])
    def quant(q, p, i): run("v", lambda: g.vector.quantize_mx(ap(q), ap(p), ap(i)), [i], [q, p])
    def mm(out, a, asc, b, bsc): run("t", lambda: g.tensor.matmul_mx(ap(out), ap(a), ap(asc), ap(b), ap(bsc), True, True), [a, asc, b, bsc], [out])
    def act(out, i): run("s", lambda: g.scalar.activation(ap(out), ap(i), AF.Copy), [i], [out])
    def actm(out, i, k): run("s", lambda: g.scalar.activation(ap(out), ap(i), AF.Copy, scale=k), [i], [out])
    def actf(out, i, f, k, c): run("s", lambda: g.scalar.activation(ap(out), ap(i), f, bias=sc(c), scale=k), [i] + rd(c), [out])
    def acti(out, i, off): run("s", lambda: g.scalar.activation(ap(out), ind(i, off), AF.Copy), [i, off], [out])
    def pick(q, p, i, ip, off):
        run("v", lambda: g.vector.tensor_copy(ap(q).bitcast(dt.uint32), ap(i).bitcast(dt.uint32).indirect(ap(off))), [i, off], [q])
        acti(p, ip, off)
    def iota(out, pattern, base, cm): run("g", lambda: g.iota(ap(out), pattern, base, cm), [], [out])
    def iotaf(out, pattern, base, cm): run("g", lambda: g.iota(ap(out), pattern, base, cm, allow_small_or_imprecise_dtypes=True), [], [out])
    def keep(out, i, pattern, op, base, cm): run("g", lambda: g.affine_select(ap(out), ap(i), pattern, op, 0.0, base, cm), [i], [out])
    ndma = [0]

    def dma(pairs, reads, writes):
        s = "d%d" % ndma[0]
        ndma[0] += 1
        for q in sorted({p[0] for p in pairs}): settle(q, reads, writes)
        for q, o, i in pairs: eng[q].dma_start(o, i).then_inc(T.sem[s], 16)
        count[s] = 16 * len(pairs)
        note(pairs[0][0], reads, writes, s, count[s])

    def send(k, t):
        s, d, kind, n = SENT[k]
        dst, src = T.cores[(rank + STEP[t]) % N], "%s%d" % (s, t)
        settle("g", [B(src)], [])
        i, o = T[src][:, 0:n], T["%s%d" % (d, t)][:, :]
        if kind == F4: i, o = i.bitcast(dt.uint8), o.bitcast(dt.uint8)
        ls, to = "l_%s%d" % (s[1], t), topo.addr(dst)
        g.remote_dma(o, i, T.sem["r_%s%d" % (s[1], t)], T.sem[ls], to[1], to[0], topo.mask(core, dst))
        count[ls] = len(topo.engines(core, dst))

    def expect(k, t):
        s, d, kind, n = SENT[k]
        rs = "r_%s%d" % (s[1], t)
        count[rs] = len(topo.engines(T.cores[(rank - STEP[t]) % N], core))
        note("far", [], [B("%s%d" % (d, t))], rs, count[rs])

    def body(name, b): return B(name, C * b, C * b + C)
    def side(name, b): return B(name, 128 * b, 128 * b + 128)
    def bank(ps, b, n=C): return B(ps, 512 * b, 512 * b + n)

    dma([("y", T.ca[:, 0:48], T.cd[:, :])], [], [B("ca", 0, 48)])
    dma([("s", T.ut[:, :], T.u[:, :])], [], [B("ut")])
    dma([("y", T.xt0[:, :], T.x[:, :])], [], [B("xt0")])
    settle("y", [B("xt0")], [])
    dma([("y", T.wq[:, :].bitcast(dt.uint8), T.wc[:, :])], [], [B("wq")])
    dma([("y", T.wp[:, :], T.ws[:, :])], [], [B("wp")])
    dma([("y", T.vt[:, :], T.v[:, :])], [], [B("vt")])

    iota(B("pi"), [[0, 1]], 0, 1)
    for s, n, p, b in PATTERNS: iota(L(s), p, b, 0)
    fill(B("one"), 1.0)
    fill(B("zero"), 0.0)
    for k, n in enumerate((15, 16, 1)): ts(B("pm", k, k + 1), B("pi"), n, OP.bitwise_and)
    copy(B("lu"), L("lu"))
    copy(B("fc"), B("pm"))
    pm, po, odd = B("fc", 0, 1), B("fc", 1, 2), B("fc", 2, 3)
    mh, up = B("mh"), B("up384")
    ts(mh, pm, odd, OP.subtract, 0.5, OP.mult)
    ts(up, po, C / 16, OP.mult)
    ts(B("ca", 48, 72), L("lnat"), 16.0, OP.mult, pm, OP.add)
    ts(B("m24"), pm, float(Q), OP.mult)
    ts(B("t1"), odd, 16.0, OP.mult, mh, OP.add)
    ts(B("lrun"), L("lrun"), mh, OP.add, pm, OP.add)
    ts(B("even"), odd, -1.0, OP.mult, 1.0, OP.add)
    ts(B("z1"), po, 4.0, OP.mult, B("t1"), OP.add)
    ts(B("lnat"), L("lnat"), B("m24"), OP.add)
    ts(B("t2"), B("even"), 64.0, OP.mult, mh, OP.add)
    ts(B("lpair", 0, 4), L("lpair"), B("z1"), OP.add)
    ts(B("lpair", 4, 8), L("lpair"), B("t2"), OP.add, po, OP.add)
    ts(B("lc", 48, 72), L("lown"), pm, OP.add, po, OP.add)
    keep(B("et"), B("one"), [[1, 516]], OP.is_equal, -3, -4)
    iotaf(B("i6"), [[1, 24], [32, 16]], 16, 0)
    iotaf(B("ia"), [[0, 24], [1, 16]], 0, 0)

    ts(B("k1"), B("ca"), 1 / Q, OP.mult, -0.479, OP.add)
    ts(B("k3"), B("ca"), 16.0, OP.mult, up, OP.add)
    ts(B("k2"), B("k1"), -383.0, OP.mult)
    quant(B("uq"), B("up"), B("ut"))
    tt(B("cb"), B("k2"), B("k3"), OP.add)
    pick(B("urq"), B("urp"), B("uq"), B("up"), B("lu"))
    copyi(B("b1"), B("cb", 0, 48), B("lrun"))
    ts(B("fr"), pm, 0.0, OP.is_equal, 385.0, OP.mult)
    for b in (0, 1): quant(side("eq", b), side("ep", b), B("et", 3 - b, 515 - b))
    turn(B("b2"), B("b1"))
    ts(B("fs"), L("first"), pm, OP.add)
    for b in (2, 3): quant(side("eq", b), side("ep", b), B("et", 3 - b, 515 - b))
    copyi(B("b1"), B("b2"), B("lpair"))
    act(B("tbl", C, 400), B("zero"))
    actf(B("tbl", 386, 387), B("zero", 0, 1), AF.Identity, 1.0, 1.0)
    actf(B("tbl", 0, C), B("i6"), AF.Identity, UNIT, 1.0)
    actf(B("tbl", 400, 800), B("tbl", 0, 400), AF.Identity, 1.0, 1.0)
    act(B("y1", 0, 16), B("zero"))
    quant(B("xq"), B("xp"), B("xt0"))
    pick(B("tq0"), B("tp0"), B("xq"), B("xp"), B("lnat"))

    def lists_of_candidates():
        ts(B("kb"), B("b1", 0, 112), B("even"), OP.mult)
        ts(B("kc"), B("b1", 16, 128), odd, OP.mult)
        tt(B("kd"), B("kb"), B("kc"), OP.add)
        copy(B("lc", 0, 48), B("kd", 0, 48))
        ts(B("ke"), B("kd", 64, 112), up, OP.subtract)
        ts(B("ke", 0, 2), B("ke", 0, 2), B("fr"), OP.add)

    def lists_inside():
        k2, k3 = B("k2", 0, 48), B("k3", 0, 48)
        levels = [[lambda: ts(k2, B("ke"), 15, OP.bitwise_and), lambda: tt(B("sel", 96, 144), B("ke"), B("fs"), OP.is_equal)],
                  [lambda: ts(B("kf"), k2, pm, OP.is_equal, 386.0, OP.mult), lambda: ts(B("ks"), B("sel", 96, 144), 400.0, OP.mult)],
                  [lambda: tt(B("kt"), B("kf"), B("ke"), OP.max), lambda: ts(B("sel", 144, 192), B("ke"), C - 1.0, OP.min)],
                  [lambda: tt(B("sel", 48, 96), B("kt"), B("ks"), OP.max), lambda: ts(k3, B("ke"), 16.0, OP.add)],
                  [lambda: ts(B("kg"), B("sel", 48, 96), 386.0, OP.is_equal, 1000.0, OP.mult)],
                  [lambda: tt(B("sel", 0, 48), B("kg"), k3, OP.min)],
                  [lambda: tt(B("sel", 0, 192, 2), B("sel", 0, 192, 2), B("sel", 1, 192, 2), OP.subtract)]]
        jobs.extend([lambda fs=fs: [f() for f in fs] for fs in levels])

    def late_constants():
        actm(B("sk", 0, 192, 2), B("one", 0, 96), 0.0)
        actf(B("ib"), B("ia", 0, 16), AF.Abs, -1.0, pm)
        actm(B("y1", 400, YW), B("one", 0, YW - 400), 0.0)
        actf(B("dg"), B("ib"), AF.Relu, -1.0, 1.0)
        keep(B("r10"), B("one", 0, 150), [[0, 15], [1, 10]], OP.not_equal, 0, 0)
        keep(B("rq"), B("one", 0, 128), [[0, 4], [1, 32]], OP.not_equal, 0, 0)
        keep(B("r9"), B("one", 0, 216), [[0, 24], [1, 9]], OP.not_equal, 0, 0)
        actf(B("rs"), B("ia"), AF.Sign, 1.0, 0.0)
        actm(B("high"), po, 1 / 16)
        for name in ("d2", "of"): act(B(name, 0, 16), B("zero"))
        act(B("rp", A, 4 * RW, RW), B("zero", 0, 4))
        act(B("tv", 7, 8), B("zero", 0, 1))
        actf(B("sign"), B("high"), AF.Identity, -2.0, 1.0)
        actf(B("low"), B("high"), AF.Identity, -1.0, 1.0)
        actf(B("rq", 31, 128, 32), B("zero", 0, 4), AF.Identity, 1.0, B("low"))

    def leave(k):
        for q in (k // 16, k // 16 + 1):
            ts(B("e1", q, 240, 16) if q < 16 else B("e1", 234 + q, 400, 10), B("y1", 17 + 16 * q, 32 + 16 * q), B("dg", q % 16, q % 16 + 1), OP.mult)

    def settled(m):
        ts(B("e2", m, C, 16), B("d2", 16 + 32 * m, 40 + 32 * m), B("dg", m, m + 1), OP.mult)

    def unpack(ps, q, p):
        for b in range(4): mm(bank(ps, b), side("eq", b), side("ep", b), B(q), B(p))

    jobs = []

    def slot():
        if jobs: jobs.pop(0)()

    def rebuild(t):
        aq, apl, al = "aq%d" % t, "ap%d" % t, "al%d" % t
        def made(b, d, a=0, e=C): return B("gm", C * (4 * b + d) + a, C * (4 * b + d) + e)
        def near(b, d, a=0, e=C): return B("mg", C * (4 * (d % 2) + b) + a, C * (4 * (d % 2) + b) + e)
        def half(ps, b, h): return B(ps, 512 * b + h, 512 * b + h + 192)
        def wait(n): jobs.extend([lambda: None] * n)

        def columns():
            for x in range(2): expect(x, t)
            unpack("psA", aq, apl)
            for b in range(4): act(B("ft", b, 4 * C, 4), bank("psA", b))

        def roots(h):
            quant(B("fq", h, h + 192), B("fz", h, h + 192), B("ft", 4 * h, 4 * h + 768))
            if h:
                unpack("psB", "fq", "fz")
                expect(2, t)
                for b in range(4): acti(near(b, 0), B("ft"), B(al, Q * b + Q, Q * b + 2 * Q))
                for b in range(4): act(made(b, 0), bank("psB", b))
                for b in range(4):
                    if b not in WHOLE[0]: acti(near(b, 1), made(b, 0), B(al, 0, Q))

        def pack(h):
            quant(B("pq", h, h + 192), B("pz", h, h + 192), B("pt", 4 * h, 4 * h + 768))
            if h:
                unpack("psB", "pq", "pz")
                for b in sorted(set(sum(WHOLE, ()))): act(body("md", b), bank("psB", b))

        def step(d, b, h):
            if b in WHOLE[d - 1]: tti(made(b, d, h, h + 192), made(b, d - 1), B(al, h // 16, h // 16 + 12), B("md", C * b + h, C * b + h + 192), OP.add)
            else: tt(made(b, d, h, h + 192), near(b, d, h, h + 192), half("psB", b, h), OP.add)
            if h and d < 3 and b not in WHOLE[d]: acti(near(b, d + 1), made(b, d), B(al, 0, Q))

        columns()
        if t == 0:
            jobs.extend([lambda: fill(B("dm"), 9.0), lambda: ts(B("t3"), odd, B("high"), OP.not_equal, A + 16.0, OP.mult),
                         lambda: ts(B("t4"), B("ca", 48, 50), 16.0, OP.mult, B("t3"), OP.add), lambda: ts(B("lsel"), B("t4"), 2.0 * A, OP.min),
                         lambda: ts(B("lback"), B("cb", 48, 72), up, OP.subtract)])
        wait(WAIT[0] - len(jobs))
        jobs.extend([lambda h=h: roots(h) for h in (0, 192)])
        wait(WAIT[1])
        jobs.extend([lambda b=b, h=h: tt(B("pt", 4 * h + b, 4 * h + 768, 4), half("psA", b, h), near(b, 0, h, h + 192), OP.subtract)
                     for b in range(4) for h in (0, 192)])
        jobs.extend([lambda h=h: pack(h) for h in (0, 192)])
        for d in (1, 2, 3):
            wait(WAIT[d + 1])
            jobs.extend([lambda d=d, b=b, h=h: step(d, b, h) for b in range(4) for h in (0, 192)])

    for t in range(R):
        tq, tp, aq, apl, al, ao = ["%s%d" % (s, t) for s in ("tq", "tp", "aq", "ap", "al", "ao")]
        if t:
            for h in (0, 192): quant(B(tq, h, h + 192), B(tp, h, h + 192), B("xt", 4 * h, 4 * h + 768))
        for k in range(4):
            h, o = 192 * (k // 2), k % 2
            mm(bank("psA", k, 192), side("urq", o), side("urp", o), B(tq, h, h + 192), B(tp, h, h + 192))
            if k < 3: act(B("sb", C * o + h, C * o + h + 192), bank("psA", k, 192))
        send(0, t)
        send(1, t)
        if t == 0: lists_of_candidates()
        copy(B("sb", C + 192, 2 * C), bank("psA", 3, 192))
        if t == 0: lists_inside()
        for k in (1, 2): acti(B("c1", C * k, C * k + C), B("sb"), B("lc", Q * k, Q * k + Q))
        slot()
        copyi(B("c1", 0, C), B("sb"), B("lc", 0, Q))
        if t == 0: late_constants()
        unpack("psB", tq, tp)
        for b in range(4): act(body("fp", b), bank("psB", b))
        for k in range(3):
            slot()
            turn(B("c2", C * k, C * k + C), B("c1", C * k, C * k + C))
        slot()
        for h in (0, 1): tt(B("da", 24 * h, 24 * h + 24), B("c2", 16 * h, 768, 32), B("c2", 768, 1152, 16), OP.subtract)
        for h in (0, 1): tt(B("db", 24 * h, 24 * h + 24), B("c2", 768, 1152, 16), B("c2", 16 * h, 768, 32), OP.subtract)
        slot()
        tt(B("dc"), B("da"), B("db"), OP.max)
        slot()
        for h in range(0, 192, 48): tt(B("sk", h + 1, h + 48, 2), B("dc", 24, 48), B("dc", 0, 24), OP.is_lt)
        scan(B("sx", 0, 144), B("sk", 0, 144), B("sel", 0, 144))
        scan(B("sx", 144, 192), B("sk", 144, 192), B("sel", 144, 192))
        for h in (1, 0): scan(B("sy", 24 * h, 24 * h + 24), B("sx", 97, 144, 2), B("sx", 48 * h + 1, 48 * h + 48, 2))
        copy(B("ql%d" % t, 0, Q), B("sx", 145, 192, 2))
        for b in (0, 1): ts(B("ql%d" % t, Q * b + Q, Q * b + 2 * Q), B("sx", 145, 192, 2), 4.0, OP.mult, float(b), OP.add)
        copy(B("lie", 0, 48), B("sy"))
        for b in (2, 3): ts(B("ql%d" % t, Q * b + Q, Q * b + 2 * Q), B("sx", 145, 192, 2), 4.0, OP.mult, float(b), OP.add)
        send(2, t)
        copy(B("lie", 48, 49), B("sy", 23, 24))
        copyi(B("y1", 16, 80), B("tbl"), B("lie", 24, 28))
        for x, y in ((4, 10), (10, 24)): acti(B("y1", 16 + 16 * x, 16 + 16 * y), B("tbl"), B("lie", 24 + x, 24 + y))
        if t == 0: iotaf(B("jt"), [[1, 4 * C]], 0, 0)
        rebuild(t)
        for k in range(32, C, 32):
            if k == C - 32:
                for s in (0, 1): tsi(B("e1", 248 + s, 408, 10), B("y1", 0, 16 + k), B("lie", 22 + 26 * s, 23 + 26 * s), B("dg", 6 + s, 7 + s))
            else:
                tti(B("y1", 16 + k, 48 + k), B("y1", 0, 16 + k), B("lie", k // 16, k // 16 + 2), B("y1", 16 + k, 48 + k), OP.add)
            leave(k - 32)
            if k == 224: leave(C - 32)
            if k == 288: scan(B("c2", 0, 240), B("rs", 0, 240), B("e1", 0, 240))
            elif k == 320: ts(B("lb", 0, 30, 2), B("c2", 15, 240, 16), 1 / UNIT, OP.mult)
            else: slot()
        tti(B("y1", 16 + k, 48 + k), B("y1", 0, 16 + k), B("lie", k // 16, k // 16 + 2), B("y1", 16 + k, 48 + k), OP.add)
        scan(B("c2", 240, 390), B("r10"), B("e1", 250, 400))
        slot()
        copy(B("d2", 16, 48), B("y1", 16, YW, 16))
        ts(B("lb", 1, 30, 2), B("c2", 249, 390, 10), 1 / UNIT, OP.mult)
        ts(B("e2", M - 1, C, 16), B("y1", 15 + M, 400, 16), B("dg", M - 1, M), OP.mult)
        for m in range(1, M - 1):
            tti(B("d2", 16 + 32 * m, 48 + 32 * m), B("d2", 0, 16 + 32 * m), B("lb", 2 * m - 2, 2 * m), B("y1", 16 + m, YW, 16), OP.add)
            settled(m - 1)
            slot()
        settled(M - 2)
        tsi(B("dl"), B("d2", 0, 496), B("lb", 28, 30), B("dg", M - 1, M))
        slot()
        scan(B("c2", 0, C), B("rs", 0, C), B("e2"))
        slot()
        tt(B("dw"), B("c2", 15, C, 16), B("dl", 0, 24), OP.add)
        slot()
        ts(B("dm", 0, 24), B("dw"), 3, OP.bitwise_and)
        slot()
        for c in range(4): ts(B("ind", 32 * c, 32 * c + 32), B("dm"), float(c), OP.is_equal)
        ts(B("ls"), B("dm", 0, 24), float(C), OP.mult)
        scan(B("inc"), B("rq"), B("ind"))
        tt(B("pos"), B("ls"), B("ca", 48, 72), OP.add)
        if MORE[0]: slot()
        turn(B("tv", 8, 136), B("inc"))
        copy(B("lv"), B("pos"))
        acti(B("jv"), B("jt"), B("lv"))
        tt(B("pr"), B("ind"), B("inc"), OP.mult)
        scan(B("bs"), B("one", 0, 128), B("tv", 7, 135))
        tt(B("ps_"), B("pr", 0, 64), B("pr", 64, 128), OP.add)
        if MORE[1]: slot()
        turn(B("tw"), B("bs"))
        tt(B("pu", 8, 216, 9), B("ps_", 0, 24), B("ps_", 32, 56), OP.add)
        if MORE[2]: slot()
        for c in range(8):
            x = 32 * (c // 2)
            ts(B("pu", c, 216, 9), B("ind", x, x + 24), B("tw", x + 30 + c % 2, x + 31 + c % 2), OP.mult, B("sign" if c % 2 else "high"), OP.mult)
        slot()
        scan(B("pv"), B("r9"), B("pu"))
        slot()
        ts(B("lpl"), B("pv", 8, 216, 9), -1.0, OP.add)
        ts(B("lpx"), B("pv", 8, 216, 9), -1.0, OP.add, float(A), OP.min)
        if MORE[3]: slot()
        run("v", lambda: g.vector.tensor_copy(ind(B("of", 16), B("lpl")), ap(B("jv"))), [B("jv"), B("lpl")], [B("of", 16)])
        slot()
        turn(B("og", 0, A), B("of", 16, 16 + A))
        turn(B("og", A), B("of", 0, A + 32))
        slot()
        copyi(B("qo%d" % t), B("og"), B("lsel"))
        send(3, t)
        while jobs: slot()
        mm(bank("psB", 3), side("eq", 3), side("ep", 3), B(tq), B(tp))
        expect(3, t)
        for b in range(4): (copyi if b % 2 else acti)(B("mt", b, 4 * A, 4), B("gm", 4 * C * b, 4 * C * b + 4 * C), B(ao))
        for h, ps in ((0, "psA"), (160, "psB")):
            quant(B("mq", h, h + 160), B("mp", h, h + 160), B("mt", 4 * h, 4 * h + 640))
            mm(B(ps, 0, 160), side("wq", 0), side("wp", 0), B("mq", h, h + 160), B("mp", h, h + 160))
            actm(B("rp", h, h + 160), B(ps, 0, 160), 0.015625)
        if t == R - 1: quant(B("vq"), B("vp"), B("vt"))
        for b in range(1, 4):
            mm(bank("psA", b, A), side("wq", b), side("wp", b), B("mq"), B("mp"))
            actm(B("rp", RW * b, RW * b + A), bank("psA", b, A), 0.015625)
        acti(B("rg"), B("rp", RW * 3, RW * 3 + A + 1), B("lpx"))
        for b in range(3): tti(B("xt", b, 4 * C, 4), B("rp", RW * b, RW * b + A + 1), B("lpx"), body("fp", b), OP.add)
        tt(B("xt", 3, 4 * C, 4), B("rg"), bank("psB", 3), OP.add)

    quant(B("tq%d" % R), B("tp%d" % R), B("xt"))
    for h in (0, 192): pick(B("oq", h, h + 192), B("op", h, h + 192), B("tq%d" % R), B("tp%d" % R), B("lback", h // 16, h // 16 + 12))
    for k, h in enumerate((0, 192)):
        mm(bank("psA", k, 192), B("vq"), B("vp"), B("oq", h, h + 192), B("op", h, h + 192))
        (copy if k else act)(B("yo", h, h + 192), bank("psA", k, 192))
    dma([("y", T.oc[:, :], T.oq[:, :].bitcast(dt.uint8))], [B("oq")], [])
    dma([("s", T.y[:, 0:192], T.yo[:, 0:192])], [B("yo", 0, 192)], [])
    dma([("s", T.osc[4 * k:4 * k + 4, :], T.op[32 * k:32 * k + 4, :]) for k in range(4)], [B("op")], [])
    dma([("y", T.y[:, 192:C], T.yo[:, 192:C])], [B("yo", 192, C)], [])
    for s in sorted(count): g.wait_ge(T.sem[s], count[s])
